import numpy as np
import ml_dtypes


def mxq(x, axis, fmt="e4m3"):
    dtype, down = {"e4m3": (ml_dtypes.float8_e4m3fn, 7), "e5m2": (ml_dtypes.float8_e5m2, 14)}[fmt]
    v = np.moveaxis(np.asarray(x, np.float32).astype(ml_dtypes.bfloat16).astype(np.float64), axis, -1)
    blocks = v.reshape(v.shape[:-1] + (-1, 32))
    amax = np.abs(blocks).max(-1, keepdims=True)
    byte = np.maximum(np.where(amax > 0, np.frexp(amax)[1] - 1 + 127, 0) - down, 1)
    scale = np.exp2(byte - 127.0)
    codes = (blocks / scale).astype(np.float32).astype(dtype).astype(np.float64)
    return np.moveaxis((codes * scale).reshape(v.shape), -1, axis)


WIDE = False


def mx_kscale(k):
    if not WIDE:
        return np.ones(k)
    levels = np.array([10, -10, 5, -5, 0])
    if k % 512:
        return np.exp2(np.random.permutation(np.resize(levels, k // 32))).repeat(32)
    a = np.empty((k // 512, 16))
    for p in range(k // 512):
        a[p, :8] = np.random.permutation(np.resize(levels, 8))
        for g in range(8):
            far = levels[np.abs(levels - a[p, g]) >= 10]
            a[p, g + 8] = far[np.random.randint(len(far))]
    return np.exp2(a.ravel()).repeat(32)


def f64(x):
    return np.asarray(x).astype(np.float64)


def striped(idx):
    return np.tile(idx.reshape(-1, 16).T, (8, 1)).astype(np.uint16)


def unstriped(offs):
    return offs[:16].T.reshape(-1).astype(np.int64)


E2M1 = np.array([0.0, 0.5, 1.0, 1.5, 2.0, 3.0, 4.0, 6.0, -0.0, -0.5, -1.0, -1.5, -2.0, -3.0, -4.0, -6.0])


def pack_weight(w, fmt):
    k, n = w.shape
    w = f64(np.asarray(w, np.float32).astype(ml_dtypes.bfloat16)).reshape(k // 32, 32, n)
    amax = np.abs(w).max(1)
    if fmt == "e4m3":
        byte = np.frexp(amax)[1] - 1 + 127 - 7
    else:
        mant, ex = np.frexp(amax / 6.0)
        byte = np.where(mant > 0.5, ex, ex - 1) + 127
    byte = np.clip(np.where(amax > 0, byte, 1), 1, 254)
    scaled = (w * np.exp2(127.0 - byte)[:, None, :]).reshape(k, n).astype(np.float32)
    by_word = np.ascontiguousarray(scaled.reshape(k // 512, 128, 4, n).transpose(0, 1, 3, 2))
    if fmt == "e4m3":
        words = by_word.astype(ml_dtypes.float8_e4m3fn).view(np.uint8)
    else:
        c = by_word.astype(ml_dtypes.float4_e2m1fn).view(np.uint8) & 0xF
        words = (c[..., 0::2] | (c[..., 1::2] << 4)).reshape(k // 512, 128, 2 * n)
    return np.ascontiguousarray(words), np.ascontiguousarray(byte.astype(np.uint8).reshape(k // 512, 16, n))


def unpack_weight(words, scales, fmt):
    g, _, n = scales.shape
    words = np.ascontiguousarray(words).reshape(g, 128, n, -1)
    if fmt == "e4m3":
        vals = words.view(ml_dtypes.float8_e4m3fn).astype(np.float64)
    else:
        nib = np.empty((g, 128, n, 4), np.uint8)
        nib[..., 0::2] = words & 0xF
        nib[..., 1::2] = words >> 4
        vals = E2M1[nib]
    vals = vals * np.repeat(np.exp2(scales.astype(np.float64) - 127.0), 8, axis=1)[..., None]
    return vals.transpose(0, 1, 3, 2).reshape(g * 512, n)


K, M, T, S = 512, 128, 4096, 2048


def setup_inputs():
    n = np.random.standard_normal
    s = mx_kscale(K)[:, None]
    s2 = mx_kscale(512)[:, None]
    v = pack_weight(n((K, T)) * s, "e4m3")
    p_w4 = pack_weight(n((K, M)) / np.sqrt(K) / s, "e2m1")
    return {
        "tab_words": v[0],
        "tab_scales": v[1],
        "w4_words": p_w4[0],
        "w4_scales": p_w4[1],
        "c": (n((512, S)) * s2).astype(np.float32),
        "u": (n((512, M)) / np.sqrt(512) / s2).astype(np.float32),
        "rT": n((M, T)).astype(np.float32),
        "b": (0.3 * n(128)).astype(np.float32),
        "offs": striped(np.random.permutation(T)[:S]),
    }


def reference(tab_words, tab_scales, w4_words, w4_scales, c, u, rT, b, offs):
    tab_ = unpack_weight(tab_words, tab_scales, "e4m3")[:, unstriped(offs)]
    w4_ = unpack_weight(w4_words, w4_scales, "e2m1")
    c_ = mxq(f64(c), 0, "e4m3")
    u_ = mxq(f64(u), 0, "e4m3")
    y = w4_.T @ tab_ + u_.T @ c_
    return (y + f64(b)[:, None]) + f64(rT)[:, unstriped(offs)]

@@ -1,0 +1,127 @@
+from contextlib import ExitStack
+
+import concourse.mybir as mybir
+
+K, M, T, S = 512, 128, 4096, 2048
+FLOPS = 2 * 2 * K * M * S
+
+F32 = mybir.dt.float32
+BF16 = mybir.dt.bfloat16
+I32 = mybir.dt.int32
+U32 = mybir.dt.uint32
+U16 = mybir.dt.uint16
+U8 = mybir.dt.uint8
+FP8X4 = mybir.dt.float8_e4m3fn_x4
+FP4X4 = mybir.dt.float4_e2m1fn_x4
+ADD = mybir.AluOpType.add
+
+P = 128
+PACK = 4
+
+LOADS = [(0, 512), (512, 512), (1024, 512), (1536, 256), (1792, 256)]
+GROUPS = [(0, 512, "s"), (512, 512, "s"), (1024, 512, "s"), (1536, 128, "s"), (1664, 128, "v"), (1792, 128, "v"), (1920, 128, "s")]
+STORES = [(0, 1024), (1024, 512), (1536, 256), (1792, 256)]
+
+
+def interleave(eng_copy, dst, src):
+    eng_copy(
+        dst.rearrange("p (c i) t -> p c t i", i=4),
+        src.rearrange("p t (c i) -> p c t i", i=4),
+    )
+
+
+def tile_list_tabres_bias_kernel(tc, tab_words, tab_scales, w4_words, w4_scales, c, u, rT, b, offs, out):
+    nc = tc.nc
+    with ExitStack() as ctx:
+        keep = ctx.enter_context(tc.tile_pool(name="keep", bufs=1))
+        psum = ctx.enter_context(tc.psum_pool(name="psum", bufs=1))
+
+        offsets = keep.tile([P, S // 16], U16, name="offsets")
+        tab_w = keep.tile([P, T], I32, name="tab_w", align_bytes=64)
+        tab_s = keep.tile([P, T // 4], I32, name="tab_s", align_bytes=64)
+        res = keep.tile([P, T], F32, name="res", align_bytes=64)
+        w4_w = keep.tile([P, 2 * M // 4], I32, name="w4_w", align_bytes=64)
+        w4_s = keep.tile([P, M // 4], I32, name="w4_s", align_bytes=64)
+        bias = keep.tile([P, 1], F32, name="bias")
+        u_raw = keep.tile([P, PACK, M], F32, name="u_raw", align_bytes=64)
+        u_bf = keep.tile([P, M, PACK], BF16, name="u_bf", align_bytes=64)
+        u_w = keep.tile([P, M], U32, name="u_w", align_bytes=64)
+        u_s = keep.tile([P, M], U8, name="u_s", align_bytes=64)
+        g_w = keep.tile([P, S], U32, name="g_w", align_bytes=64)
+        g_s = keep.tile([P, S], U8, name="g_s", align_bytes=64)
+        g_r = keep.tile([P, S], F32, name="g_r", align_bytes=64)
+        result = keep.tile([P, S], F32, name="result", align_bytes=64)
+        c_raw = [keep.tile([P, PACK, w], F32, name="c_raw%d" % i, align_bytes=64) for i, (c0, w) in enumerate(LOADS)]
+        c_bf = [keep.tile([P, w, PACK], BF16, name="c_bf%d" % i, align_bytes=64) for i, (c0, w, e) in enumerate(GROUPS)]
+        c_w = keep.tile([P, S], U32, name="c_w", align_bytes=64)
+        c_s = keep.tile([P, S], U8, name="c_s", align_bytes=64)
+        acc = [psum.tile([P, w], F32, name="acc%d" % i) for i, (c0, w, e) in enumerate(GROUPS)]
+
+        nc.vector.memset(tab_s[:], 0)
+        nc.vector.memset(w4_s[:], 0)
+
+        nc.sync.dma_start(offsets[:], offs)
+        nc.sync.dma_start(u_raw[:], u.rearrange("(p j) n -> p j n", j=PACK))
+        nc.sync.dma_start(w4_w[:], w4_words[0].bitcast(I32))
+        ts_rows = tab_scales[0].bitcast(I32)
+        for r in range(4):
+            nc.sync.dma_start(tab_s[r:P:32, :], ts_rows[r:16:4, :])
+        nc.sync.dma_start(tab_w[:], tab_words[0].rearrange("p t i -> p (t i)").bitcast(I32))
+        nc.sync.dma_start(bias[:], b.rearrange("(p o) -> p o", o=1))
+        ws_rows = w4_scales[0].bitcast(I32)
+        for r in range(4):
+            nc.sync.dma_start(w4_s[r:P:32, :], ws_rows[r:16:4, :])
+        nc.sync.dma_start(res[:], rT)
+        c_rows = c.rearrange("(p j) s -> p j s", j=PACK)
+        for i, (c0, w) in enumerate(LOADS):
+            nc.sync.dma_start(c_raw[i][:], c_rows[:, :, c0 : c0 + w])
+
+        interleave(nc.scalar.copy, u_bf[:], u_raw[:])
+
+        nc.vector.tensor_copy(g_s[:], tab_s[:].bitcast(U8).indirect(offsets[:]))
+        nc.vector.quantize_mx(u_w[:].bitcast(FP8X4), u_s[:], u_bf[:].rearrange("p n t -> p (n t)"))
+        nc.vector.tensor_copy(g_w[:], tab_w[:].bitcast(U32).indirect(offsets[:]))
+        nc.vector.tensor_copy(g_r[:], res[:].indirect(offsets[:]))
+
+        w4_codes = w4_w[:].bitcast(U8).bitcast(FP4X4)
+        w4_scale = w4_s[:].bitcast(U8)
+        for g, (c0, w, e) in enumerate(GROUPS):
+            nc.tensor.matmul_mx(
+                acc[g][:], lhsT=w4_codes, lhsT_scale=w4_scale,
+                rhs=g_w[:, c0 : c0 + w].bitcast(FP8X4), rhs_scale=g_s[:, c0 : c0 + w],
+                start=True, stop=False,
+            )
+
+        def cast(g):
+            c0, w, e = GROUPS[g]
+            i = max(k for k, (l0, lw) in enumerate(LOADS) if l0 <= c0)
+            src = c_raw[i][:, :, c0 - LOADS[i][0] : c0 - LOADS[i][0] + w]
+            interleave(nc.scalar.copy if e == "s" else nc.vector.tensor_copy, c_bf[g][:], src)
+
+        def quant(g):
+            c0, w, e = GROUPS[g]
+            nc.vector.quantize_mx(
+                c_w[:, c0 : c0 + w].bitcast(FP8X4), c_s[:, c0 : c0 + w], c_bf[g][:].rearrange("p n t -> p (n t)")
+            )
+            nc.tensor.matmul_mx(
+                acc[g][:], lhsT=u_w[:].bitcast(FP8X4), lhsT_scale=u_s[:],
+                rhs=c_w[:, c0 : c0 + w].bitcast(FP8X4), rhs_scale=c_s[:, c0 : c0 + w],
+                start=False, stop=True,
+            )
+
+        def finish(g):
+            c0, w, e = GROUPS[g]
+            nc.vector.scalar_tensor_tensor(
+                result[:, c0 : c0 + w], acc[g][:], bias[:], g_r[:, c0 : c0 + w], ADD, ADD
+            )
+            for s0, sw in STORES:
+                if s0 + sw == c0 + w:
+                    nc.sync.dma_start(out[:, s0 : s0 + sw], result[:, s0 : s0 + sw])
+
+        for step in range(len(GROUPS) + 2):
+            if step < len(GROUPS):
+                cast(step)
+            if 1 <= step <= len(GROUPS):
+                quant(step - 1)
+            if step >= 2:
+                finish(step - 2)

@@ -18,16 +18,14 @@ ADD = mybir.AluOpType.add
 P = 128
 PACK = 4
 
-LOADS = [(0, 512), (512, 512), (1024, 512), (1536, 256), (1792, 256)]
-GROUPS = [(0, 512, "s"), (512, 512, "s"), (1024, 512, "s"), (1536, 128, "s"), (1664, 128, "v"), (1792, 128, "v"), (1920, 128, "s")]
-STORES = [(0, 1024), (1024, 512), (1536, 256), (1792, 256)]
+MULT = mybir.AluOpType.mult
+LOADS = [(0, 512, 512), (512, 512, 288), (1024, 512, 288), (1536, 256, 256), (1792, 256, 144)]
+GROUPS = [(0, 512), (512, 512), (1024, 512), (1536, 128), (1664, 128), (1792, 128), (1920, 128)]
+ORDER = ["q0", "q1", "a0", "a1", "q2", "q3", "a2", "q4", "a3", "a4", "a5", "a6"]
 
 
-def interleave(eng_copy, dst, src):
-    eng_copy(
-        dst.rearrange("p (c i) t -> p c t i", i=4),
-        src.rearrange("p t (c i) -> p c t i", i=4),
-    )
+def blocks(dst, src):
+    return dst.rearrange("p (c i) t -> p c t i", i=4), src.rearrange("p t (c i) -> p c t i", i=4)
 
 
 def tile_list_tabres_bias_kernel(tc, tab_words, tab_scales, w4_words, w4_scales, c, u, rT, b, offs, out):
@@ -51,11 +49,11 @@ def tile_list_tabres_bias_kernel(tc, tab_words, tab_scales, w4_words, w4_scales,
         g_s = keep.tile([P, S], U8, name="g_s", align_bytes=64)
         g_r = keep.tile([P, S], F32, name="g_r", align_bytes=64)
         result = keep.tile([P, S], F32, name="result", align_bytes=64)
-        c_raw = [keep.tile([P, PACK, w], F32, name="c_raw%d" % i, align_bytes=64) for i, (c0, w) in enumerate(LOADS)]
-        c_bf = [keep.tile([P, w, PACK], BF16, name="c_bf%d" % i, align_bytes=64) for i, (c0, w, e) in enumerate(GROUPS)]
+        c_raw = [keep.tile([P, PACK, w], F32, name="c_raw%d" % i, align_bytes=64) for i, (c0, w, e) in enumerate(LOADS)]
+        c_bf = [keep.tile([P, w, PACK], BF16, name="c_bf%d" % i, align_bytes=64) for i, (c0, w, e) in enumerate(LOADS)]
         c_w = keep.tile([P, S], U32, name="c_w", align_bytes=64)
         c_s = keep.tile([P, S], U8, name="c_s", align_bytes=64)
-        acc = [psum.tile([P, w], F32, name="acc%d" % i) for i, (c0, w, e) in enumerate(GROUPS)]
+        acc = [psum.tile([P, w], F32, name="acc%d" % i) for i, (c0, w) in enumerate(GROUPS)]
 
         nc.vector.memset(tab_s[:], 0)
         nc.vector.memset(w4_s[:], 0)
@@ -73,10 +71,10 @@ def tile_list_tabres_bias_kernel(tc, tab_words, tab_scales, w4_words, w4_scales,
             nc.sync.dma_start(w4_s[r:P:32, :], ws_rows[r:16:4, :])
         nc.sync.dma_start(res[:], rT)
         c_rows = c.rearrange("(p j) s -> p j s", j=PACK)
-        for i, (c0, w) in enumerate(LOADS):
+        for i, (c0, w, e) in enumerate(LOADS):
             nc.sync.dma_start(c_raw[i][:], c_rows[:, :, c0 : c0 + w])
 
-        interleave(nc.scalar.copy, u_bf[:], u_raw[:])
+        nc.scalar.copy(*blocks(u_bf[:], u_raw[:]))
 
         nc.vector.tensor_copy(g_s[:], tab_s[:].bitcast(U8).indirect(offsets[:]))
         nc.vector.quantize_mx(u_w[:].bitcast(FP8X4), u_s[:], u_bf[:].rearrange("p n t -> p (n t)"))
@@ -85,43 +83,42 @@ def tile_list_tabres_bias_kernel(tc, tab_words, tab_scales, w4_words, w4_scales,
 
         w4_codes = w4_w[:].bitcast(U8).bitcast(FP4X4)
         w4_scale = w4_s[:].bitcast(U8)
-        for g, (c0, w, e) in enumerate(GROUPS):
+        for g, (c0, w) in enumerate(GROUPS):
             nc.tensor.matmul_mx(
                 acc[g][:], lhsT=w4_codes, lhsT_scale=w4_scale,
                 rhs=g_w[:, c0 : c0 + w].bitcast(FP8X4), rhs_scale=g_s[:, c0 : c0 + w],
                 start=True, stop=False,
             )
 
-        def cast(g):
-            c0, w, e = GROUPS[g]
-            i = max(k for k, (l0, lw) in enumerate(LOADS) if l0 <= c0)
-            src = c_raw[i][:, :, c0 - LOADS[i][0] : c0 - LOADS[i][0] + w]
-            interleave(nc.scalar.copy if e == "s" else nc.vector.tensor_copy, c_bf[g][:], src)
+        for i, (c0, w, e) in enumerate(LOADS):
+            nc.scalar.copy(*blocks(c_bf[i][:, 0:e, :], c_raw[i][:, :, 0:e]))
+            if e < w:
+                nc.gpsimd.tensor_scalar(*blocks(c_bf[i][:, e:w, :], c_raw[i][:, :, e:w]), 1.0, 0.0, MULT, ADD)
 
-        def quant(g):
-            c0, w, e = GROUPS[g]
+        def quant(i):
+            l0, lw, e = LOADS[i]
             nc.vector.quantize_mx(
-                c_w[:, c0 : c0 + w].bitcast(FP8X4), c_s[:, c0 : c0 + w], c_bf[g][:].rearrange("p n t -> p (n t)")
+                c_w[:, l0 : l0 + lw].bitcast(FP8X4), c_s[:, l0 : l0 + lw], c_bf[i][:].rearrange("p n t -> p (n t)")
             )
-            nc.tensor.matmul_mx(
-                acc[g][:], lhsT=u_w[:].bitcast(FP8X4), lhsT_scale=u_s[:],
-                rhs=c_w[:, c0 : c0 + w].bitcast(FP8X4), rhs_scale=c_s[:, c0 : c0 + w],
-                start=False, stop=True,
-            )
+            for g, (c0, w) in enumerate(GROUPS):
+                if l0 <= c0 < l0 + lw:
+                    nc.tensor.matmul_mx(
+                        acc[g][:], lhsT=u_w[:].bitcast(FP8X4), lhsT_scale=u_s[:],
+                        rhs=c_w[:, c0 : c0 + w].bitcast(FP8X4), rhs_scale=c_s[:, c0 : c0 + w],
+                        start=False, stop=True,
+                    )
 
         def finish(g):
-            c0, w, e = GROUPS[g]
+            c0, w = GROUPS[g]
             nc.vector.scalar_tensor_tensor(
                 result[:, c0 : c0 + w], acc[g][:], bias[:], g_r[:, c0 : c0 + w], ADD, ADD
             )
-            for s0, sw in STORES:
+            for s0, sw, e in LOADS:
                 if s0 + sw == c0 + w:
                     nc.sync.dma_start(out[:, s0 : s0 + sw], result[:, s0 : s0 + sw])
 
-        for step in range(len(GROUPS) + 2):
-            if step < len(GROUPS):
-                cast(step)
-            if 1 <= step <= len(GROUPS):
-                quant(step - 1)
-            if step >= 2:
-                finish(step - 2)
+        for step in ORDER:
+            if step[0] == "q":
+                quant(int(step[1]))
+            else:
+                finish(int(step[1]))

@@ -19,9 +19,11 @@ P = 128
 PACK = 4
 
 MULT = mybir.AluOpType.mult
-LOADS = [(0, 512, 512), (512, 512, 288), (1024, 512, 288), (1536, 256, 256), (1792, 256, 144)]
-GROUPS = [(0, 512), (512, 512), (1024, 512), (1536, 128), (1664, 128), (1792, 128), (1920, 128)]
-ORDER = ["q0", "q1", "a0", "a1", "q2", "q3", "a2", "q4", "a3", "a4", "a5", "a6"]
+LOADS = [(0, 512, 512), (512, 512, 288), (1024, 256, 256), (1280, 256, 256), (1536, 256, 256), (1792, 128, 0), (1920, 128, 128)]
+GROUPS = [(0, 512), (512, 512)] + [(1024 + 128 * g, 128) for g in range(8)]
+STORES = [(0, 512), (512, 512), (1024, 512), (1536, 256), (1792, 256)]
+REUSE = {0: 1, 512: 2, 1024: 3, 1536: 6}
+ORDER = ["q0", "q1", "a0", "o8", "q2", "a1", "o9", "q3", "a2", "a3", "a4", "a5", "q4", "q5", "q6", "a6", "a7", "a8", "a9"]
 
 
 def blocks(dst, src):
@@ -48,12 +50,11 @@ def tile_list_tabres_bias_kernel(tc, tab_words, tab_scales, w4_words, w4_scales,
         g_w = keep.tile([P, S], U32, name="g_w", align_bytes=64)
         g_s = keep.tile([P, S], U8, name="g_s", align_bytes=64)
         g_r = keep.tile([P, S], F32, name="g_r", align_bytes=64)
-        result = keep.tile([P, S], F32, name="result", align_bytes=64)
-        c_raw = [keep.tile([P, PACK, w], F32, name="c_raw%d" % i, align_bytes=64) for i, (c0, w, e) in enumerate(LOADS)]
+        c_raw = [keep.tile([P, PACK, w], F32, name="c_raw%d" % i, tag="stage%d" % i, align_bytes=64) for i, (c0, w, e) in enumerate(LOADS)]
         c_bf = [keep.tile([P, w, PACK], BF16, name="c_bf%d" % i, align_bytes=64) for i, (c0, w, e) in enumerate(LOADS)]
         c_w = keep.tile([P, S], U32, name="c_w", align_bytes=64)
         c_s = keep.tile([P, S], U8, name="c_s", align_bytes=64)
-        acc = [psum.tile([P, w], F32, name="acc%d" % i) for i, (c0, w) in enumerate(GROUPS)]
+        acc = {}
 
         nc.vector.memset(tab_s[:], 0)
         nc.vector.memset(w4_s[:], 0)
@@ -83,15 +84,22 @@ def tile_list_tabres_bias_kernel(tc, tab_words, tab_scales, w4_words, w4_scales,
 
         w4_codes = w4_w[:].bitcast(U8).bitcast(FP4X4)
         w4_scale = w4_s[:].bitcast(U8)
-        for g, (c0, w) in enumerate(GROUPS):
+
+        def open_group(g):
+            c0, w = GROUPS[g]
+            acc[g] = psum.tile([P, w], F32, name="acc%d" % g, tag="bank%d" % (g % 8))
             nc.tensor.matmul_mx(
                 acc[g][:], lhsT=w4_codes, lhsT_scale=w4_scale,
                 rhs=g_w[:, c0 : c0 + w].bitcast(FP8X4), rhs_scale=g_s[:, c0 : c0 + w],
                 start=True, stop=False,
             )
 
+        for g in range(8):
+            open_group(g)
+
         for i, (c0, w, e) in enumerate(LOADS):
-            nc.scalar.copy(*blocks(c_bf[i][:, 0:e, :], c_raw[i][:, :, 0:e]))
+            if e > 0:
+                nc.scalar.copy(*blocks(c_bf[i][:, 0:e, :], c_raw[i][:, :, 0:e]))
             if e < w:
                 nc.gpsimd.tensor_scalar(*blocks(c_bf[i][:, e:w, :], c_raw[i][:, :, e:w]), 1.0, 0.0, MULT, ADD)
 
@@ -108,17 +116,24 @@ def tile_list_tabres_bias_kernel(tc, tab_words, tab_scales, w4_words, w4_scales,
                         start=False, stop=True,
                     )
 
+        result = {}
+
         def finish(g):
             c0, w = GROUPS[g]
+            r0 = c0 // 512 * 512
+            if c0 == r0:
+                result[r0] = keep.tile([P, 512], F32, name="result%d" % r0, tag="stage%d" % REUSE[r0], align_bytes=64)
             nc.vector.scalar_tensor_tensor(
-                result[:, c0 : c0 + w], acc[g][:], bias[:], g_r[:, c0 : c0 + w], ADD, ADD
+                result[r0][:, c0 - r0 : c0 - r0 + w], acc[g][:], bias[:], g_r[:, c0 : c0 + w], ADD, ADD
             )
-            for s0, sw, e in LOADS:
+            for s0, sw in STORES:
                 if s0 + sw == c0 + w:
-                    nc.sync.dma_start(out[:, s0 : s0 + sw], result[:, s0 : s0 + sw])
+                    nc.sync.dma_start(out[:, s0 : s0 + sw], result[r0][:, s0 - r0 : s0 - r0 + sw])
 
         for step in ORDER:
             if step[0] == "q":
                 quant(int(step[1]))
+            elif step[0] == "o":
+                open_group(int(step[1]))
             else:
                 finish(int(step[1]))

@@ -18,12 +18,10 @@ ADD = mybir.AluOpType.add
 P = 128
 PACK = 4
 
-MULT = mybir.AluOpType.mult
-LOADS = [(0, 512, 512), (512, 512, 288), (1024, 256, 256), (1280, 256, 256), (1536, 256, 256), (1792, 128, 0), (1920, 128, 128)]
-GROUPS = [(0, 512), (512, 512)] + [(1024 + 128 * g, 128) for g in range(8)]
-STORES = [(0, 512), (512, 512), (1024, 512), (1536, 256), (1792, 256)]
-REUSE = {0: 1, 512: 2, 1024: 3, 1536: 6}
-ORDER = ["q0", "q1", "a0", "o8", "q2", "a1", "o9", "q3", "a2", "a3", "a4", "a5", "q4", "q5", "q6", "a6", "a7", "a8", "a9"]
+
+LOADS = [256] * 6 + [128] * 4
+STEPS = [2] + [1] * 8
+VCAST = {}
 
 
 def blocks(dst, src):
@@ -50,8 +48,12 @@ def tile_list_tabres_bias_kernel(tc, tab_words, tab_scales, w4_words, w4_scales,
         g_w = keep.tile([P, S], U32, name="g_w", align_bytes=64)
         g_s = keep.tile([P, S], U8, name="g_s", align_bytes=64)
         g_r = keep.tile([P, S], F32, name="g_r", align_bytes=64)
-        c_raw = [keep.tile([P, PACK, w], F32, name="c_raw%d" % i, tag="stage%d" % i, align_bytes=64) for i, (c0, w, e) in enumerate(LOADS)]
-        c_bf = [keep.tile([P, w, PACK], BF16, name="c_bf%d" % i, align_bytes=64) for i, (c0, w, e) in enumerate(LOADS)]
+        c_raw = [keep.tile([P, PACK * w], F32, name="c_raw%d" % i, align_bytes=64) for i, w in enumerate(LOADS)]
+        load0 = [sum(LOADS[:i]) for i in range(len(LOADS))]
+        first = [sum(STEPS[:s]) for s in range(len(STEPS))]
+        width = [sum(LOADS[first[s] : first[s] + STEPS[s]]) for s in range(len(STEPS))]
+        col0 = [load0[first[s]] for s in range(len(STEPS))]
+        c_bf = [keep.tile([P, w, PACK], BF16, name="c_bf%d" % s, align_bytes=64) for s, w in enumerate(width)]
         c_w = keep.tile([P, S], U32, name="c_w", align_bytes=64)
         c_s = keep.tile([P, S], U8, name="c_s", align_bytes=64)
         acc = {}
@@ -72,8 +74,8 @@ def tile_list_tabres_bias_kernel(tc, tab_words, tab_scales, w4_words, w4_scales,
             nc.sync.dma_start(w4_s[r:P:32, :], ws_rows[r:16:4, :])
         nc.sync.dma_start(res[:], rT)
         c_rows = c.rearrange("(p j) s -> p j s", j=PACK)
-        for i, (c0, w, e) in enumerate(LOADS):
-            nc.sync.dma_start(c_raw[i][:], c_rows[:, :, c0 : c0 + w])
+        for i, w in enumerate(LOADS):
+            nc.sync.dma_start(c_raw[i][:].rearrange("p (j s) -> p j s", j=PACK), c_rows[:, :, load0[i] : load0[i] + w])
 
         nc.scalar.copy(*blocks(u_bf[:], u_raw[:]))
 
@@ -85,55 +87,54 @@ def tile_list_tabres_bias_kernel(tc, tab_words, tab_scales, w4_words, w4_scales,
         w4_codes = w4_w[:].bitcast(U8).bitcast(FP4X4)
         w4_scale = w4_s[:].bitcast(U8)
 
-        def open_group(g):
-            c0, w = GROUPS[g]
-            acc[g] = psum.tile([P, w], F32, name="acc%d" % g, tag="bank%d" % (g % 8))
-            nc.tensor.matmul_mx(
-                acc[g][:], lhsT=w4_codes, lhsT_scale=w4_scale,
-                rhs=g_w[:, c0 : c0 + w].bitcast(FP8X4), rhs_scale=g_s[:, c0 : c0 + w],
-                start=True, stop=False,
-            )
+        def open_group(s):
+            c0, w = col0[s], width[s]
+            acc[s] = psum.tile([P, w], F32, name="acc%d" % s, tag="bank%d" % (s % 8))
+            n = w if w == 512 else 128
+            for a in range(0, w, n):
+                nc.tensor.matmul_mx(
+                    acc[s][:, a : a + n], lhsT=w4_codes, lhsT_scale=w4_scale,
+                    rhs=g_w[:, c0 + a : c0 + a + n].bitcast(FP8X4), rhs_scale=g_s[:, c0 + a : c0 + a + n],
+                    start=a == 0, stop=False,
+                )
 
-        for g in range(8):
-            open_group(g)
+        def cast(s):
+            for i in range(first[s], first[s] + STEPS[s]):
+                w = LOADS[i]
+                a = load0[i] - col0[s]
+                e = w - VCAST.get(i, 0)
+                raw = c_raw[i][:].rearrange("p (j s) -> p j s", j=PACK)
+                if e > 0:
+                    nc.scalar.copy(*blocks(c_bf[s][:, a : a + e, :], raw[:, :, 0:e]))
+                if e < w:
+                    nc.vector.tensor_copy(*blocks(c_bf[s][:, a + e : a + w, :], raw[:, :, e:w]))
 
-        for i, (c0, w, e) in enumerate(LOADS):
-            if e > 0:
-                nc.scalar.copy(*blocks(c_bf[i][:, 0:e, :], c_raw[i][:, :, 0:e]))
-            if e < w:
-                nc.gpsimd.tensor_scalar(*blocks(c_bf[i][:, e:w, :], c_raw[i][:, :, e:w]), 1.0, 0.0, MULT, ADD)
-
-        def quant(i):
-            l0, lw, e = LOADS[i]
+        def quant(s):
+            c0, w = col0[s], width[s]
             nc.vector.quantize_mx(
-                c_w[:, l0 : l0 + lw].bitcast(FP8X4), c_s[:, l0 : l0 + lw], c_bf[i][:].rearrange("p n t -> p (n t)")
+                c_w[:, c0 : c0 + w].bitcast(FP8X4), c_s[:, c0 : c0 + w], c_bf[s][:].rearrange("p n t -> p (n t)")
             )
-            for g, (c0, w) in enumerate(GROUPS):
-                if l0 <= c0 < l0 + lw:
-                    nc.tensor.matmul_mx(
-                        acc[g][:], lhsT=u_w[:].bitcast(FP8X4), lhsT_scale=u_s[:],
-                        rhs=c_w[:, c0 : c0 + w].bitcast(FP8X4), rhs_scale=c_s[:, c0 : c0 + w],
-                        start=False, stop=True,
-                    )
-
-        result = {}
-
-        def finish(g):
-            c0, w = GROUPS[g]
-            r0 = c0 // 512 * 512
-            if c0 == r0:
-                result[r0] = keep.tile([P, 512], F32, name="result%d" % r0, tag="stage%d" % REUSE[r0], align_bytes=64)
-            nc.vector.scalar_tensor_tensor(
-                result[r0][:, c0 - r0 : c0 - r0 + w], acc[g][:], bias[:], g_r[:, c0 : c0 + w], ADD, ADD
+            nc.tensor.matmul_mx(
+                acc[s][:], lhsT=u_w[:].bitcast(FP8X4), lhsT_scale=u_s[:],
+                rhs=c_w[:, c0 : c0 + w].bitcast(FP8X4), rhs_scale=c_s[:, c0 : c0 + w],
+                start=False, stop=True,
             )
-            for s0, sw in STORES:
-                if s0 + sw == c0 + w:
-                    nc.sync.dma_start(out[:, s0 : s0 + sw], result[r0][:, s0 - r0 : s0 - r0 + sw])
 
-        for step in ORDER:
-            if step[0] == "q":
-                quant(int(step[1]))
-            elif step[0] == "o":
-                open_group(int(step[1]))
-            else:
-                finish(int(step[1]))
+        def finish(s):
+            c0, w = col0[s], width[s]
+            last = s == len(STEPS) - 1
+            host = c_raw[first[s] if last else first[s + 1]]
+            a = w if last else 0
+            nc.vector.scalar_tensor_tensor(host[:, a : a + w], acc[s][:], bias[:], g_r[:, c0 : c0 + w], ADD, ADD)
+            nc.sync.dma_start(out[:, c0 : c0 + w], host[:, a : a + w])
+
+        for s in range(min(8, len(STEPS))):
+            open_group(s)
+        for s in range(len(STEPS)):
+            cast(s)
+            quant(s)
+            if s > 0:
+                finish(s - 1)
+                if s + 7 < len(STEPS):
+                    open_group(s + 7)
+        finish(len(STEPS) - 1)

@@ -19,13 +19,14 @@ P = 128
 PACK = 4
 
 
-LOADS = [256] * 6 + [128] * 4
-STEPS = [2] + [1] * 8
-VCAST = {}
+LOADS = [512, 512, 256, 256, 256, 256]
+STEPS = [(0, 0, 512, 0), (1, 0, 512, 256), (2, 0, 256, 0), (3, 0, 256, 0), (4, 0, 256, 0), (5, 0, 128, 128), (5, 128, 128, 0)]
+HOSTS = [(1, 0), (2, 0), (3, 0), (4, 0), (5, 0), (5, 256), (5, 384)]
+RUN = 4
 
 
 def blocks(dst, src):
-    return dst.rearrange("p (c i) t -> p c t i", i=4), src.rearrange("p t (c i) -> p c t i", i=4)
+    return dst.rearrange("p (c i) t -> p c t i", i=RUN), src.rearrange("p t (c i) -> p c t i", i=RUN)
 
 
 def tile_list_tabres_bias_kernel(tc, tab_words, tab_scales, w4_words, w4_scales, c, u, rT, b, offs, out):
@@ -50,9 +51,8 @@ def tile_list_tabres_bias_kernel(tc, tab_words, tab_scales, w4_words, w4_scales,
         g_r = keep.tile([P, S], F32, name="g_r", align_bytes=64)
         c_raw = [keep.tile([P, PACK * w], F32, name="c_raw%d" % i, align_bytes=64) for i, w in enumerate(LOADS)]
         load0 = [sum(LOADS[:i]) for i in range(len(LOADS))]
-        first = [sum(STEPS[:s]) for s in range(len(STEPS))]
-        width = [sum(LOADS[first[s] : first[s] + STEPS[s]]) for s in range(len(STEPS))]
-        col0 = [load0[first[s]] for s in range(len(STEPS))]
+        width = [w for i, a, w, v in STEPS]
+        col0 = [load0[i] + a for i, a, w, v in STEPS]
         c_bf = [keep.tile([P, w, PACK], BF16, name="c_bf%d" % s, align_bytes=64) for s, w in enumerate(width)]
         c_w = keep.tile([P, S], U32, name="c_w", align_bytes=64)
         c_s = keep.tile([P, S], U8, name="c_s", align_bytes=64)
@@ -99,15 +99,13 @@ def tile_list_tabres_bias_kernel(tc, tab_words, tab_scales, w4_words, w4_scales,
                 )
 
         def cast(s):
-            for i in range(first[s], first[s] + STEPS[s]):
-                w = LOADS[i]
-                a = load0[i] - col0[s]
-                e = w - VCAST.get(i, 0)
-                raw = c_raw[i][:].rearrange("p (j s) -> p j s", j=PACK)
-                if e > 0:
-                    nc.scalar.copy(*blocks(c_bf[s][:, a : a + e, :], raw[:, :, 0:e]))
-                if e < w:
-                    nc.vector.tensor_copy(*blocks(c_bf[s][:, a + e : a + w, :], raw[:, :, e:w]))
+            i, a, w, v = STEPS[s]
+            e = w - v
+            raw = c_raw[i][:].rearrange("p (j s) -> p j s", j=PACK)
+            if e > 0:
+                nc.scalar.copy(*blocks(c_bf[s][:, 0:e, :], raw[:, :, a : a + e]))
+            if e < w:
+                nc.vector.tensor_copy(*blocks(c_bf[s][:, e:w, :], raw[:, :, a + e : a + w]))
 
         def quant(s):
             c0, w = col0[s], width[s]
@@ -122,19 +120,15 @@ def tile_list_tabres_bias_kernel(tc, tab_words, tab_scales, w4_words, w4_scales,
 
         def finish(s):
             c0, w = col0[s], width[s]
-            last = s == len(STEPS) - 1
-            host = c_raw[first[s] if last else first[s + 1]]
-            a = w if last else 0
+            host, a = c_raw[HOSTS[s][0]], HOSTS[s][1]
             nc.vector.scalar_tensor_tensor(host[:, a : a + w], acc[s][:], bias[:], g_r[:, c0 : c0 + w], ADD, ADD)
             nc.sync.dma_start(out[:, c0 : c0 + w], host[:, a : a + w])
 
-        for s in range(min(8, len(STEPS))):
+        for s in range(len(STEPS)):
             open_group(s)
         for s in range(len(STEPS)):
             cast(s)
+        for s in range(len(STEPS)):
             quant(s)
-            if s > 0:
-                finish(s - 1)
-                if s + 7 < len(STEPS):
-                    open_group(s + 7)
-        finish(len(STEPS) - 1)
+        for s in range(len(STEPS)):
+            finish(s)

@@ -33,11 +33,12 @@ def tile_list_tabres_bias_kernel(tc, tab_words, tab_scales, w4_words, w4_scales,
     nc = tc.nc
     with ExitStack() as ctx:
         keep = ctx.enter_context(tc.tile_pool(name="keep", bufs=1))
+        shared = ctx.enter_context(tc.tile_pool(name="shared", bufs=1))
         psum = ctx.enter_context(tc.psum_pool(name="psum", bufs=1))
 
         offsets = keep.tile([P, S // 16], U16, name="offsets")
-        tab_w = keep.tile([P, T], I32, name="tab_w", align_bytes=64)
-        tab_s = keep.tile([P, T // 4], I32, name="tab_s", align_bytes=64)
+        tab_w = shared.tile([P, T], I32, name="tab_w", align_bytes=64, offset=0)
+        tab_s = shared.tile([P, T // 4], I32, name="tab_s", align_bytes=64, offset=4 * T)
         res = keep.tile([P, T], F32, name="res", align_bytes=64)
         w4_w = keep.tile([P, 2 * M // 4], I32, name="w4_w", align_bytes=64)
         w4_s = keep.tile([P, M // 4], I32, name="w4_s", align_bytes=64)
@@ -47,9 +48,12 @@ def tile_list_tabres_bias_kernel(tc, tab_words, tab_scales, w4_words, w4_scales,
         u_w = keep.tile([P, M], U32, name="u_w", align_bytes=64)
         u_s = keep.tile([P, M], U8, name="u_s", align_bytes=64)
         g_w = keep.tile([P, S], U32, name="g_w", align_bytes=64)
-        g_s = keep.tile([P, S], U8, name="g_s", align_bytes=64)
+        g_far = keep.tile([P, S], U8, name="g_far", align_bytes=64)
+        g_words = keep.tile([P, S // 4], I32, name="g_words", align_bytes=64)
+        g_s = g_words[:].bitcast(U8)
         g_r = keep.tile([P, S], F32, name="g_r", align_bytes=64)
-        c_raw = [keep.tile([P, PACK * w], F32, name="c_raw%d" % i, align_bytes=64) for i, w in enumerate(LOADS)]
+        place = [4 * T + 4 * PACK * LOADS[1], 4 * T] + [4 * PACK * sum(LOADS[2:i]) for i in range(2, len(LOADS))]
+        c_raw = [shared.tile([P, PACK * w], F32, name="c_raw%d" % i, align_bytes=64, offset=place[i]) for i, w in enumerate(LOADS)]
         load0 = [sum(LOADS[:i]) for i in range(len(LOADS))]
         width = [w for i, a, w, v in STEPS]
         col0 = [load0[i] + a for i, a, w, v in STEPS]
@@ -60,29 +64,36 @@ def tile_list_tabres_bias_kernel(tc, tab_words, tab_scales, w4_words, w4_scales,
 
         nc.vector.memset(tab_s[:], 0)
         nc.vector.memset(w4_s[:], 0)
+        nc.vector.memset(g_words[:], 0)
+
+        c_rows = c.rearrange("(p j) s -> p j s", j=PACK)
+
+        def load_c(i):
+            w = LOADS[i]
+            nc.sync.dma_start(c_raw[i][:].rearrange("p (j s) -> p j s", j=PACK), c_rows[:, :, load0[i] : load0[i] + w])
 
         nc.sync.dma_start(offsets[:], offs)
-        nc.sync.dma_start(u_raw[:], u.rearrange("(p j) n -> p j n", j=PACK))
         nc.sync.dma_start(w4_w[:], w4_words[0].bitcast(I32))
-        ts_rows = tab_scales[0].bitcast(I32)
-        for r in range(4):
-            nc.sync.dma_start(tab_s[r:P:32, :], ts_rows[r:16:4, :])
-        nc.sync.dma_start(tab_w[:], tab_words[0].rearrange("p t i -> p (t i)").bitcast(I32))
         nc.sync.dma_start(bias[:], b.rearrange("(p o) -> p o", o=1))
+        nc.sync.dma_start(tab_s[32:96:4, :], tab_scales[0].bitcast(I32))
+        nc.sync.dma_start(tab_w[:], tab_words[0].rearrange("p t i -> p (t i)").bitcast(I32))
         ws_rows = w4_scales[0].bitcast(I32)
         for r in range(4):
             nc.sync.dma_start(w4_s[r:P:32, :], ws_rows[r:16:4, :])
         nc.sync.dma_start(res[:], rT)
-        c_rows = c.rearrange("(p j) s -> p j s", j=PACK)
-        for i, w in enumerate(LOADS):
-            nc.sync.dma_start(c_raw[i][:].rearrange("p (j s) -> p j s", j=PACK), c_rows[:, :, load0[i] : load0[i] + w])
+        nc.sync.dma_start(u_raw[:], u.rearrange("(p j) n -> p j n", j=PACK))
+        load_c(0)
 
-        nc.scalar.copy(*blocks(u_bf[:], u_raw[:]))
-
-        nc.vector.tensor_copy(g_s[:], tab_s[:].bitcast(U8).indirect(offsets[:]))
-        nc.vector.quantize_mx(u_w[:].bitcast(FP8X4), u_s[:], u_bf[:].rearrange("p n t -> p (n t)"))
+        nc.vector.tensor_copy(g_far[:], tab_s[:].bitcast(U8).indirect(offsets[:]))
+        for q in range(4):
+            nc.sync.dma_start(g_words[32 * q : 32 * q + 4, :], g_far[:].bitcast(I32)[32 + 16 * q : 48 + 16 * q : 4, :])
+        load_c(1)
         nc.vector.tensor_copy(g_w[:], tab_w[:].bitcast(U32).indirect(offsets[:]))
+        for i in range(2, len(LOADS)):
+            load_c(i)
         nc.vector.tensor_copy(g_r[:], res[:].indirect(offsets[:]))
+        nc.scalar.copy(*blocks(u_bf[:], u_raw[:]))
+        nc.vector.quantize_mx(u_w[:].bitcast(FP8X4), u_s[:], u_bf[:].rearrange("p n t -> p (n t)"))
 
         w4_codes = w4_w[:].bitcast(U8).bitcast(FP4X4)
         w4_scale = w4_s[:].bitcast(U8)

@@ -73,6 +73,7 @@ def tile_list_tabres_bias_kernel(tc, tab_words, tab_scales, w4_words, w4_scales,
             nc.sync.dma_start(c_raw[i][:].rearrange("p (j s) -> p j s", j=PACK), c_rows[:, :, load0[i] : load0[i] + w])
 
         nc.sync.dma_start(offsets[:], offs)
+        nc.sync.dma_start(u_raw[:], u.rearrange("(p j) n -> p j n", j=PACK))
         nc.sync.dma_start(w4_w[:], w4_words[0].bitcast(I32))
         nc.sync.dma_start(bias[:], b.rearrange("(p o) -> p o", o=1))
         nc.sync.dma_start(tab_s[32:96:4, :], tab_scales[0].bitcast(I32))
@@ -81,19 +82,18 @@ def tile_list_tabres_bias_kernel(tc, tab_words, tab_scales, w4_words, w4_scales,
         for r in range(4):
             nc.sync.dma_start(w4_s[r:P:32, :], ws_rows[r:16:4, :])
         nc.sync.dma_start(res[:], rT)
-        nc.sync.dma_start(u_raw[:], u.rearrange("(p j) n -> p j n", j=PACK))
         load_c(0)
 
         nc.vector.tensor_copy(g_far[:], tab_s[:].bitcast(U8).indirect(offsets[:]))
         for q in range(4):
             nc.sync.dma_start(g_words[32 * q : 32 * q + 4, :], g_far[:].bitcast(I32)[32 + 16 * q : 48 + 16 * q : 4, :])
         load_c(1)
+        nc.scalar.copy(*blocks(u_bf[:], u_raw[:]))
+        nc.vector.quantize_mx(u_w[:].bitcast(FP8X4), u_s[:], u_bf[:].rearrange("p n t -> p (n t)"))
         nc.vector.tensor_copy(g_w[:], tab_w[:].bitcast(U32).indirect(offsets[:]))
         for i in range(2, len(LOADS)):
             load_c(i)
         nc.vector.tensor_copy(g_r[:], res[:].indirect(offsets[:]))
-        nc.scalar.copy(*blocks(u_bf[:], u_raw[:]))
-        nc.vector.quantize_mx(u_w[:].bitcast(FP8X4), u_s[:], u_bf[:].rearrange("p n t -> p (n t)"))
 
         w4_codes = w4_w[:].bitcast(U8).bitcast(FP4X4)
         w4_scale = w4_s[:].bitcast(U8)

@@ -19,10 +19,10 @@ P = 128
 PACK = 4
 
 
-LOADS = [512, 512, 256, 256, 256, 256]
-STEPS = [(0, 0, 512, 0), (1, 0, 512, 256), (2, 0, 256, 0), (3, 0, 256, 0), (4, 0, 256, 0), (5, 0, 128, 128), (5, 128, 128, 0)]
-HOSTS = [(1, 0), (2, 0), (3, 0), (4, 0), (5, 0), (5, 256), (5, 384)]
-RUN = 4
+LOADS = [512, 512, 256, 256, 256, 128, 128]
+STEPS = [(0, 0, 512, 0), (1, 0, 512, 128), (2, 0, 256, 0), (3, 0, 256, 0), (4, 0, 256, 0), (5, 0, 128, 0), (6, 0, 128, 64)]
+HOSTS = [(1, 0), (2, 0), (3, 0), (4, 0), (6, 0), (6, 256), (6, 384)]
+RUN = 2
 
 
 def blocks(dst, src):
@@ -57,7 +57,8 @@ def tile_list_tabres_bias_kernel(tc, tab_words, tab_scales, w4_words, w4_scales,
         load0 = [sum(LOADS[:i]) for i in range(len(LOADS))]
         width = [w for i, a, w, v in STEPS]
         col0 = [load0[i] + a for i, a, w, v in STEPS]
-        c_bf = [keep.tile([P, w, PACK], BF16, name="c_bf%d" % s, align_bytes=64) for s, w in enumerate(width)]
+        c_bf = [keep.tile([P, w, PACK], BF16, name="c_bf%d" % s, align_bytes=64)[:] for s, w in enumerate(width[:-1])]
+        c_bf.append(c_bf[4][:, 0:128, :])
         c_w = keep.tile([P, S], U32, name="c_w", align_bytes=64)
         c_s = keep.tile([P, S], U8, name="c_s", align_bytes=64)
         acc = {}
@@ -121,7 +122,7 @@ def tile_list_tabres_bias_kernel(tc, tab_words, tab_scales, w4_words, w4_scales,
         def quant(s):
             c0, w = col0[s], width[s]
             nc.vector.quantize_mx(
-                c_w[:, c0 : c0 + w].bitcast(FP8X4), c_s[:, c0 : c0 + w], c_bf[s][:].rearrange("p n t -> p (n t)")
+                c_w[:, c0 : c0 + w].bitcast(FP8X4), c_s[:, c0 : c0 + w], c_bf[s].rearrange("p n t -> p (n t)")
             )
             nc.tensor.matmul_mx(
                 acc[s][:], lhsT=u_w[:].bitcast(FP8X4), lhsT_scale=u_s[:],
@@ -137,9 +138,13 @@ def tile_list_tabres_bias_kernel(tc, tab_words, tab_scales, w4_words, w4_scales,
 
         for s in range(len(STEPS)):
             open_group(s)
-        for s in range(len(STEPS)):
+        for s in range(5):
             cast(s)
-        for s in range(len(STEPS)):
+        for s in range(5):
+            quant(s)
+        for s in (5, 6):
+            cast(s)
+        for s in (5, 6):
             quant(s)
         for s in range(len(STEPS)):
             finish(s)

@@ -76,18 +76,18 @@ def tile_list_tabres_bias_kernel(tc, tab_words, tab_scales, w4_words, w4_scales,
         nc.sync.dma_start(offsets[:], offs)
         nc.sync.dma_start(u_raw[:], u.rearrange("(p j) n -> p j n", j=PACK))
         nc.sync.dma_start(w4_w[:], w4_words[0].bitcast(I32))
-        nc.sync.dma_start(bias[:], b.rearrange("(p o) -> p o", o=1))
         nc.sync.dma_start(tab_s[32:96:4, :], tab_scales[0].bitcast(I32))
         nc.sync.dma_start(tab_w[:], tab_words[0].rearrange("p t i -> p (t i)").bitcast(I32))
+        nc.sync.dma_start(res[:], rT)
         ws_rows = w4_scales[0].bitcast(I32)
         for r in range(4):
             nc.sync.dma_start(w4_s[r:P:32, :], ws_rows[r:16:4, :])
-        nc.sync.dma_start(res[:], rT)
+        nc.sync.dma_start(bias[:], b.rearrange("(p o) -> p o", o=1))
         load_c(0)
 
         nc.vector.tensor_copy(g_far[:], tab_s[:].bitcast(U8).indirect(offsets[:]))
-        for q in range(4):
-            nc.sync.dma_start(g_words[32 * q : 32 * q + 4, :], g_far[:].bitcast(I32)[32 + 16 * q : 48 + 16 * q : 4, :])
+        for r in range(4):
+            nc.sync.dma_start(g_words[r:P:32, :], g_far[:].bitcast(I32)[32 + 4 * r : 96 : 16, :])
         load_c(1)
         nc.scalar.copy(*blocks(u_bf[:], u_raw[:]))
         nc.vector.quantize_mx(u_w[:].bitcast(FP8X4), u_s[:], u_bf[:].rearrange("p n t -> p (n t)"))

@@ -36,31 +36,31 @@ def tile_list_tabres_bias_kernel(tc, tab_words, tab_scales, w4_words, w4_scales,
         shared = ctx.enter_context(tc.tile_pool(name="shared", bufs=1))
         psum = ctx.enter_context(tc.psum_pool(name="psum", bufs=1))
 
-        offsets = keep.tile([P, S // 16], U16, name="offsets")
-        tab_w = shared.tile([P, T], I32, name="tab_w", align_bytes=64, offset=0)
-        tab_s = shared.tile([P, T // 4], I32, name="tab_s", align_bytes=64, offset=4 * T)
-        res = keep.tile([P, T], F32, name="res", align_bytes=64)
-        w4_w = keep.tile([P, 2 * M // 4], I32, name="w4_w", align_bytes=64)
-        w4_s = keep.tile([P, M // 4], I32, name="w4_s", align_bytes=64)
-        bias = keep.tile([P, 1], F32, name="bias")
-        u_raw = keep.tile([P, PACK, M], F32, name="u_raw", align_bytes=64)
-        u_bf = keep.tile([P, M, PACK], BF16, name="u_bf", align_bytes=64)
-        u_w = keep.tile([P, M], U32, name="u_w", align_bytes=64)
-        u_s = keep.tile([P, M], U8, name="u_s", align_bytes=64)
-        g_w = keep.tile([P, S], U32, name="g_w", align_bytes=64)
-        g_far = keep.tile([P, S], U8, name="g_far", align_bytes=64)
-        g_words = keep.tile([P, S // 4], I32, name="g_words", align_bytes=64)
+        offsets = keep.tile([P, S // 16], U16, name="offsets", align_bytes=256)
+        tab_w = shared.tile([P, T], I32, name="tab_w", align_bytes=256, offset=0)
+        tab_s = shared.tile([P, T // 4], I32, name="tab_s", align_bytes=256, offset=4 * T)
+        res = keep.tile([P, T], F32, name="res", align_bytes=256)
+        w4_w = keep.tile([P, 2 * M // 4], I32, name="w4_w", align_bytes=256)
+        w4_s = keep.tile([P, M // 4], I32, name="w4_s", align_bytes=256)
+        bias = keep.tile([P, 1], F32, name="bias", align_bytes=256)
+        u_raw = keep.tile([P, PACK, M], F32, name="u_raw", align_bytes=256)
+        u_bf = keep.tile([P, M, PACK], BF16, name="u_bf", align_bytes=256)
+        u_w = keep.tile([P, M], U32, name="u_w", align_bytes=256)
+        u_s = keep.tile([P, M], U8, name="u_s", align_bytes=256)
+        g_w = keep.tile([P, S], U32, name="g_w", align_bytes=256)
+        g_far = keep.tile([P, S], U8, name="g_far", align_bytes=256)
+        g_words = keep.tile([P, S // 4], I32, name="g_words", align_bytes=256)
         g_s = g_words[:].bitcast(U8)
-        g_r = keep.tile([P, S], F32, name="g_r", align_bytes=64)
+        g_r = keep.tile([P, S], F32, name="g_r", align_bytes=256)
         place = [4 * T + 4 * PACK * LOADS[1], 4 * T] + [4 * PACK * sum(LOADS[2:i]) for i in range(2, len(LOADS))]
-        c_raw = [shared.tile([P, PACK * w], F32, name="c_raw%d" % i, align_bytes=64, offset=place[i]) for i, w in enumerate(LOADS)]
+        c_raw = [shared.tile([P, PACK * w], F32, name="c_raw%d" % i, align_bytes=256, offset=place[i]) for i, w in enumerate(LOADS)]
         load0 = [sum(LOADS[:i]) for i in range(len(LOADS))]
         width = [w for i, a, w, v in STEPS]
         col0 = [load0[i] + a for i, a, w, v in STEPS]
-        c_bf = [keep.tile([P, w, PACK], BF16, name="c_bf%d" % s, align_bytes=64)[:] for s, w in enumerate(width[:-1])]
+        c_bf = [keep.tile([P, w, PACK], BF16, name="c_bf%d" % s, align_bytes=256)[:] for s, w in enumerate(width[:-1])]
         c_bf.append(c_bf[4][:, 0:128, :])
-        c_w = keep.tile([P, S], U32, name="c_w", align_bytes=64)
-        c_s = keep.tile([P, S], U8, name="c_s", align_bytes=64)
+        c_w = keep.tile([P, S], U32, name="c_w", align_bytes=256)
+        c_s = keep.tile([P, S], U8, name="c_s", align_bytes=256)
         acc = {}
 
         nc.vector.memset(tab_s[:], 0)

@@ -20,9 +20,11 @@ PACK = 4
 
 
 LOADS = [512, 512, 256, 256, 256, 128, 128]
-STEPS = [(0, 0, 512, 0), (1, 0, 512, 128), (2, 0, 256, 0), (3, 0, 256, 0), (4, 0, 256, 0), (5, 0, 128, 0), (6, 0, 128, 64)]
-HOSTS = [(1, 0), (2, 0), (3, 0), (4, 0), (6, 0), (6, 256), (6, 384)]
+STEPS = [(0, 0, 512, 0), (1, 0, 512, 64), (2, 0, 256, 0), (3, 0, 256, 0), (4, 0, 256, 64), (5, 0, 128, 0), (6, 0, 128, 64)]
+HOSTS = [(1, 0), (2, 0), (3, 256), (4, 0), (6, 0), (6, 256), (6, 384)]
 RUN = 2
+FRONT = [2 * (w - v) if v else 0 for i, a, w, v in STEPS[1:]] + [0]
+PAD = sum(FRONT[2:])
 
 
 def blocks(dst, src):
@@ -37,12 +39,12 @@ def tile_list_tabres_bias_kernel(tc, tab_words, tab_scales, w4_words, w4_scales,
         psum = ctx.enter_context(tc.psum_pool(name="psum", bufs=1))
 
         offsets = keep.tile([P, S // 16], U16, name="offsets", align_bytes=256)
-        tab_w = shared.tile([P, T], I32, name="tab_w", align_bytes=256, offset=0)
-        tab_s = shared.tile([P, T // 4], I32, name="tab_s", align_bytes=256, offset=4 * T)
+        tab_w = shared.tile([P, T], I32, name="tab_w", align_bytes=256, offset=4 * PAD)
+        tab_s = shared.tile([P, T // 4], I32, name="tab_s", align_bytes=256, offset=4 * (PAD + T))
         res = keep.tile([P, T], F32, name="res", align_bytes=256)
         w4_w = keep.tile([P, 2 * M // 4], I32, name="w4_w", align_bytes=256)
         w4_s = keep.tile([P, M // 4], I32, name="w4_s", align_bytes=256)
-        bias = keep.tile([P, 1], F32, name="bias", align_bytes=256)
+        bias = shared.tile([P, 1], F32, name="bias", align_bytes=256, offset=4 * (PAD + T))
         u_raw = keep.tile([P, PACK, M], F32, name="u_raw", align_bytes=256)
         u_bf = keep.tile([P, M, PACK], BF16, name="u_bf", align_bytes=256)
         u_w = keep.tile([P, M], U32, name="u_w", align_bytes=256)
@@ -52,13 +54,19 @@ def tile_list_tabres_bias_kernel(tc, tab_words, tab_scales, w4_words, w4_scales,
         g_words = keep.tile([P, S // 4], I32, name="g_words", align_bytes=256)
         g_s = g_words[:].bitcast(U8)
         g_r = keep.tile([P, S], F32, name="g_r", align_bytes=256)
-        place = [4 * T + 4 * PACK * LOADS[1], 4 * T] + [4 * PACK * sum(LOADS[2:i]) for i in range(2, len(LOADS))]
-        c_raw = [shared.tile([P, PACK * w], F32, name="c_raw%d" % i, align_bytes=256, offset=place[i]) for i, w in enumerate(LOADS)]
+        words = [FRONT[i] + PACK * w for i, w in enumerate(LOADS)]
+        top = 4 * (PAD + T) + 256
+        place = [top + 4 * words[1], top] + [4 * sum(words[2:i]) for i in range(2, len(LOADS))]
+        c_raw = [shared.tile([P, words[i]], F32, name="c_raw%d" % i, align_bytes=256, offset=place[i]) for i, w in enumerate(LOADS)]
         load0 = [sum(LOADS[:i]) for i in range(len(LOADS))]
         width = [w for i, a, w, v in STEPS]
         col0 = [load0[i] + a for i, a, w, v in STEPS]
-        c_bf = [keep.tile([P, w, PACK], BF16, name="c_bf%d" % s, align_bytes=256)[:] for s, w in enumerate(width[:-1])]
-        c_bf.append(c_bf[4][:, 0:128, :])
+        c_bf = [
+            c_raw[s - 1][:, 0 : 2 * w].bitcast(BF16).rearrange("p (n t) -> p n t", t=PACK)
+            if v
+            else keep.tile([P, w, PACK], BF16, name="c_bf%d" % s, align_bytes=256)[:]
+            for s, (i, a, w, v) in enumerate(STEPS)
+        ]
         c_w = keep.tile([P, S], U32, name="c_w", align_bytes=256)
         c_s = keep.tile([P, S], U8, name="c_s", align_bytes=256)
         acc = {}
@@ -69,9 +77,12 @@ def tile_list_tabres_bias_kernel(tc, tab_words, tab_scales, w4_words, w4_scales,
 
         c_rows = c.rearrange("(p j) s -> p j s", j=PACK)
 
+        def planes(i):
+            return c_raw[i][:, FRONT[i] : words[i]].rearrange("p (j s) -> p j s", j=PACK)
+
         def load_c(i):
             w = LOADS[i]
-            nc.sync.dma_start(c_raw[i][:].rearrange("p (j s) -> p j s", j=PACK), c_rows[:, :, load0[i] : load0[i] + w])
+            nc.sync.dma_start(planes(i), c_rows[:, :, load0[i] : load0[i] + w])
 
         nc.sync.dma_start(offsets[:], offs)
         nc.sync.dma_start(u_raw[:], u.rearrange("(p j) n -> p j n", j=PACK))
@@ -82,13 +93,13 @@ def tile_list_tabres_bias_kernel(tc, tab_words, tab_scales, w4_words, w4_scales,
         ws_rows = w4_scales[0].bitcast(I32)
         for r in range(4):
             nc.sync.dma_start(w4_s[r:P:32, :], ws_rows[r:16:4, :])
-        nc.sync.dma_start(bias[:], b.rearrange("(p o) -> p o", o=1))
         load_c(0)
 
         nc.vector.tensor_copy(g_far[:], tab_s[:].bitcast(U8).indirect(offsets[:]))
         for r in range(4):
             nc.sync.dma_start(g_words[r:P:32, :], g_far[:].bitcast(I32)[32 + 4 * r : 96 : 16, :])
         load_c(1)
+        nc.sync.dma_start(bias[:], b.rearrange("(p o) -> p o", o=1))
         nc.scalar.copy(*blocks(u_bf[:], u_raw[:]))
         nc.vector.quantize_mx(u_w[:].bitcast(FP8X4), u_s[:], u_bf[:].rearrange("p n t -> p (n t)"))
         nc.vector.tensor_copy(g_w[:], tab_w[:].bitcast(U32).indirect(offsets[:]))
@@ -113,7 +124,7 @@ def tile_list_tabres_bias_kernel(tc, tab_words, tab_scales, w4_words, w4_scales,
         def cast(s):
             i, a, w, v = STEPS[s]
             e = w - v
-            raw = c_raw[i][:].rearrange("p (j s) -> p j s", j=PACK)
+            raw = planes(i)
             if e > 0:
                 nc.scalar.copy(*blocks(c_bf[s][:, 0:e, :], raw[:, :, a : a + e]))
             if e < w:
@@ -132,19 +143,24 @@ def tile_list_tabres_bias_kernel(tc, tab_words, tab_scales, w4_words, w4_scales,
 
         def finish(s):
             c0, w = col0[s], width[s]
-            host, a = c_raw[HOSTS[s][0]], HOSTS[s][1]
+            host, a = c_raw[HOSTS[s][0]], FRONT[HOSTS[s][0]] + HOSTS[s][1]
             nc.vector.scalar_tensor_tensor(host[:, a : a + w], acc[s][:], bias[:], g_r[:, c0 : c0 + w], ADD, ADD)
             nc.sync.dma_start(out[:, c0 : c0 + w], host[:, a : a + w])
 
         for s in range(len(STEPS)):
             open_group(s)
-        for s in range(5):
+        for s in range(4):
             cast(s)
-        for s in range(5):
+        for s in range(4):
             quant(s)
+        cast(4)
+        for s in range(3):
+            finish(s)
+        quant(4)
+        finish(3)
         for s in (5, 6):
             cast(s)
         for s in (5, 6):
             quant(s)
-        for s in range(len(STEPS)):
+        for s in range(4, len(STEPS)):
             finish(s)

@@ -19,12 +19,14 @@ P = 128
 PACK = 4
 
 
-LOADS = [512, 512, 256, 256, 256, 128, 128]
-STEPS = [(0, 0, 512, 0), (1, 0, 512, 64), (2, 0, 256, 0), (3, 0, 256, 0), (4, 0, 256, 64), (5, 0, 128, 0), (6, 0, 128, 64)]
-HOSTS = [(1, 0), (2, 0), (3, 256), (4, 0), (6, 0), (6, 256), (6, 384)]
+LOADS = [512, 384, 384, 256, 256, 128, 128]
+STEPS = [512, 512, 256, 256, 256, 128, 128]
+SHARE = [0, 128, 0, 0, 64, 0, 0]
+HOSTS = [(2, 0), (3, 256), (4, 0), (6, 0), (6, 256), (5, 0), (5, 128)]
 RUN = 2
-FRONT = [2 * (w - v) if v else 0 for i, a, w, v in STEPS[1:]] + [0]
-PAD = sum(FRONT[2:])
+HELD = 4
+FRONT = [2 * (STEPS[HELD] - SHARE[HELD]) if i == HELD - 1 else 0 for i in range(len(LOADS))]
+PAD = sum(FRONT[2:]) + PACK * sum(LOADS[2:]) - T
 
 
 def blocks(dst, src):
@@ -59,13 +61,13 @@ def tile_list_tabres_bias_kernel(tc, tab_words, tab_scales, w4_words, w4_scales,
         place = [top + 4 * words[1], top] + [4 * sum(words[2:i]) for i in range(2, len(LOADS))]
         c_raw = [shared.tile([P, words[i]], F32, name="c_raw%d" % i, align_bytes=256, offset=place[i]) for i, w in enumerate(LOADS)]
         load0 = [sum(LOADS[:i]) for i in range(len(LOADS))]
-        width = [w for i, a, w, v in STEPS]
-        col0 = [load0[i] + a for i, a, w, v in STEPS]
+        width = STEPS
+        col0 = [sum(STEPS[:s]) for s in range(len(STEPS))]
         c_bf = [
             c_raw[s - 1][:, 0 : 2 * w].bitcast(BF16).rearrange("p (n t) -> p n t", t=PACK)
-            if v
+            if s == HELD
             else keep.tile([P, w, PACK], BF16, name="c_bf%d" % s, align_bytes=256)[:]
-            for s, (i, a, w, v) in enumerate(STEPS)
+            for s, w in enumerate(STEPS)
         ]
         c_w = keep.tile([P, S], U32, name="c_w", align_bytes=256)
         c_s = keep.tile([P, S], U8, name="c_s", align_bytes=256)
@@ -122,13 +124,13 @@ def tile_list_tabres_bias_kernel(tc, tab_words, tab_scales, w4_words, w4_scales,
                 )
 
         def cast(s):
-            i, a, w, v = STEPS[s]
-            e = w - v
-            raw = planes(i)
-            if e > 0:
-                nc.scalar.copy(*blocks(c_bf[s][:, 0:e, :], raw[:, :, a : a + e]))
-            if e < w:
-                nc.vector.tensor_copy(*blocks(c_bf[s][:, e:w, :], raw[:, :, a + e : a + w]))
+            c0 = col0[s]
+            cut = c0 + width[s] - SHARE[s]
+            for copy, lo, hi in ((nc.scalar.copy, c0, cut), (nc.vector.tensor_copy, cut, c0 + width[s])):
+                for i, w in enumerate(LOADS):
+                    a, e = max(lo, load0[i]), min(hi, load0[i] + w)
+                    if a < e:
+                        copy(*blocks(c_bf[s][:, a - c0 : e - c0, :], planes(i)[:, :, a - load0[i] : e - load0[i]]))
 
         def quant(s):
             c0, w = col0[s], width[s]
@@ -151,16 +153,17 @@ def tile_list_tabres_bias_kernel(tc, tab_words, tab_scales, w4_words, w4_scales,
             open_group(s)
         for s in range(4):
             cast(s)
-        for s in range(4):
-            quant(s)
-        cast(4)
         for s in range(3):
-            finish(s)
+            quant(s)
+        finish(0)
+        quant(3)
+        cast(4)
+        finish(1)
         quant(4)
-        finish(3)
+        finish(2)
         for s in (5, 6):
             cast(s)
         for s in (5, 6):
             quant(s)
-        for s in range(4, len(STEPS)):
+        for s in range(3, len(STEPS)):
             finish(s)

@@ -17,16 +17,13 @@ ADD = mybir.AluOpType.add
 
 P = 128
 PACK = 4
-
-
-LOADS = [512, 384, 384, 256, 256, 128, 128]
-STEPS = [512, 512, 256, 256, 256, 128, 128]
-SHARE = [0, 128, 0, 0, 64, 0, 0]
-HOSTS = [(2, 0), (3, 256), (4, 0), (6, 0), (6, 256), (5, 0), (5, 128)]
 RUN = 2
-HELD = 4
-FRONT = [2 * (STEPS[HELD] - SHARE[HELD]) if i == HELD - 1 else 0 for i in range(len(LOADS))]
-PAD = sum(FRONT[2:]) + PACK * sum(LOADS[2:]) - T
+
+LOADS = [256] * 8
+STEPS = [256, 512, 512, 256, 256, 128, 128]
+SHARE = [0, 0, 0, 0, 64, 0, 0]
+HOSTS = [(2, 0), (5, 0), (5, 512), (6, 0), (7, 256), (7, 640), (7, 896)]
+LAG = 2
 
 
 def blocks(dst, src):
@@ -40,13 +37,21 @@ def tile_list_tabres_bias_kernel(tc, tab_words, tab_scales, w4_words, w4_scales,
         shared = ctx.enter_context(tc.tile_pool(name="shared", bufs=1))
         psum = ctx.enter_context(tc.psum_pool(name="psum", bufs=1))
 
+        size = [4 * PACK * w for w in LOADS]
+        at_s = size[2] - 1024
+        at_w = at_s + 2048 + size[3]
+        late = [at_w + sum(size[4:i]) for i in range(4, len(LOADS))]
+        at_0 = max(at_w + 4 * T, late[-1] + size[-1])
+        place = [at_0, at_0 + size[0], 0, at_s + 2048] + late
+
         offsets = keep.tile([P, S // 16], U16, name="offsets", align_bytes=256)
-        tab_w = shared.tile([P, T], I32, name="tab_w", align_bytes=256, offset=4 * PAD)
-        tab_s = shared.tile([P, T // 4], I32, name="tab_s", align_bytes=256, offset=4 * (PAD + T))
+        tab_w = shared.tile([P, T], I32, name="tab_w", align_bytes=256, offset=at_w)
+        tab_s = shared.tile([P, T // 4], I32, name="tab_s", align_bytes=256, offset=at_s)
+        w4_s = keep.tile([P, M // 4], I32, name="w4_s", align_bytes=256)
+        bias = shared.tile([P, 1], F32, name="bias", align_bytes=256, offset=at_s + 1280)
+        c_raw = [shared.tile([P, PACK * w], F32, name="c_raw%d" % i, align_bytes=256, offset=place[i]) for i, w in enumerate(LOADS)]
         res = keep.tile([P, T], F32, name="res", align_bytes=256)
         w4_w = keep.tile([P, 2 * M // 4], I32, name="w4_w", align_bytes=256)
-        w4_s = keep.tile([P, M // 4], I32, name="w4_s", align_bytes=256)
-        bias = shared.tile([P, 1], F32, name="bias", align_bytes=256, offset=4 * (PAD + T))
         u_raw = keep.tile([P, PACK, M], F32, name="u_raw", align_bytes=256)
         u_bf = keep.tile([P, M, PACK], BF16, name="u_bf", align_bytes=256)
         u_w = keep.tile([P, M], U32, name="u_w", align_bytes=256)
@@ -56,19 +61,9 @@ def tile_list_tabres_bias_kernel(tc, tab_words, tab_scales, w4_words, w4_scales,
         g_words = keep.tile([P, S // 4], I32, name="g_words", align_bytes=256)
         g_s = g_words[:].bitcast(U8)
         g_r = keep.tile([P, S], F32, name="g_r", align_bytes=256)
-        words = [FRONT[i] + PACK * w for i, w in enumerate(LOADS)]
-        top = 4 * (PAD + T) + 256
-        place = [top + 4 * words[1], top] + [4 * sum(words[2:i]) for i in range(2, len(LOADS))]
-        c_raw = [shared.tile([P, words[i]], F32, name="c_raw%d" % i, align_bytes=256, offset=place[i]) for i, w in enumerate(LOADS)]
         load0 = [sum(LOADS[:i]) for i in range(len(LOADS))]
-        width = STEPS
         col0 = [sum(STEPS[:s]) for s in range(len(STEPS))]
-        c_bf = [
-            c_raw[s - 1][:, 0 : 2 * w].bitcast(BF16).rearrange("p (n t) -> p n t", t=PACK)
-            if s == HELD
-            else keep.tile([P, w, PACK], BF16, name="c_bf%d" % s, align_bytes=256)[:]
-            for s, w in enumerate(STEPS)
-        ]
+        c_bf = [keep.tile([P, w, PACK], BF16, name="c_bf%d" % s, align_bytes=256) for s, w in enumerate(STEPS)]
         c_w = keep.tile([P, S], U32, name="c_w", align_bytes=256)
         c_s = keep.tile([P, S], U8, name="c_s", align_bytes=256)
         acc = {}
@@ -80,7 +75,7 @@ def tile_list_tabres_bias_kernel(tc, tab_words, tab_scales, w4_words, w4_scales,
         c_rows = c.rearrange("(p j) s -> p j s", j=PACK)
 
         def planes(i):
-            return c_raw[i][:, FRONT[i] : words[i]].rearrange("p (j s) -> p j s", j=PACK)
+            return c_raw[i][:].rearrange("p (j s) -> p j s", j=PACK)
 
         def load_c(i):
             w = LOADS[i]
@@ -91,30 +86,31 @@ def tile_list_tabres_bias_kernel(tc, tab_words, tab_scales, w4_words, w4_scales,
         nc.sync.dma_start(w4_w[:], w4_words[0].bitcast(I32))
         nc.sync.dma_start(tab_s[32:96:4, :], tab_scales[0].bitcast(I32))
         nc.sync.dma_start(tab_w[:], tab_words[0].rearrange("p t i -> p (t i)").bitcast(I32))
-        nc.sync.dma_start(res[:], rT)
         ws_rows = w4_scales[0].bitcast(I32)
         for r in range(4):
             nc.sync.dma_start(w4_s[r:P:32, :], ws_rows[r:16:4, :])
         load_c(0)
+        nc.sync.dma_start(res[:], rT)
+        load_c(1)
 
         nc.vector.tensor_copy(g_far[:], tab_s[:].bitcast(U8).indirect(offsets[:]))
         for r in range(4):
             nc.sync.dma_start(g_words[r:P:32, :], g_far[:].bitcast(I32)[32 + 4 * r : 96 : 16, :])
-        load_c(1)
+        load_c(2)
+        load_c(3)
         nc.sync.dma_start(bias[:], b.rearrange("(p o) -> p o", o=1))
         nc.scalar.copy(*blocks(u_bf[:], u_raw[:]))
         nc.vector.quantize_mx(u_w[:].bitcast(FP8X4), u_s[:], u_bf[:].rearrange("p n t -> p (n t)"))
         nc.vector.tensor_copy(g_w[:], tab_w[:].bitcast(U32).indirect(offsets[:]))
-        for i in range(2, len(LOADS)):
+        for i in range(4, len(LOADS)):
             load_c(i)
-        nc.vector.tensor_copy(g_r[:], res[:].indirect(offsets[:]))
 
         w4_codes = w4_w[:].bitcast(U8).bitcast(FP4X4)
         w4_scale = w4_s[:].bitcast(U8)
 
         def open_group(s):
-            c0, w = col0[s], width[s]
-            acc[s] = psum.tile([P, w], F32, name="acc%d" % s, tag="bank%d" % (s % 8))
+            c0, w = col0[s], STEPS[s]
+            acc[s] = psum.tile([P, w], F32, name="acc%d" % s, tag="bank%d" % s)
             n = w if w == 512 else 128
             for a in range(0, w, n):
                 nc.tensor.matmul_mx(
@@ -125,18 +121,21 @@ def tile_list_tabres_bias_kernel(tc, tab_words, tab_scales, w4_words, w4_scales,
 
         def cast(s):
             c0 = col0[s]
-            cut = c0 + width[s] - SHARE[s]
-            for copy, lo, hi in ((nc.scalar.copy, c0, cut), (nc.vector.tensor_copy, cut, c0 + width[s])):
+            cut = c0 + STEPS[s] - SHARE[s]
+            for copy, lo, hi in ((nc.scalar.copy, c0, cut), (nc.vector.tensor_copy, cut, c0 + STEPS[s])):
                 for i, w in enumerate(LOADS):
                     a, e = max(lo, load0[i]), min(hi, load0[i] + w)
                     if a < e:
                         copy(*blocks(c_bf[s][:, a - c0 : e - c0, :], planes(i)[:, :, a - load0[i] : e - load0[i]]))
 
         def quant(s):
-            c0, w = col0[s], width[s]
+            c0, w = col0[s], STEPS[s]
             nc.vector.quantize_mx(
-                c_w[:, c0 : c0 + w].bitcast(FP8X4), c_s[:, c0 : c0 + w], c_bf[s].rearrange("p n t -> p (n t)")
+                c_w[:, c0 : c0 + w].bitcast(FP8X4), c_s[:, c0 : c0 + w], c_bf[s][:].rearrange("p n t -> p (n t)")
             )
+
+        def close(s):
+            c0, w = col0[s], STEPS[s]
             nc.tensor.matmul_mx(
                 acc[s][:], lhsT=u_w[:].bitcast(FP8X4), lhsT_scale=u_s[:],
                 rhs=c_w[:, c0 : c0 + w].bitcast(FP8X4), rhs_scale=c_s[:, c0 : c0 + w],
@@ -144,26 +143,28 @@ def tile_list_tabres_bias_kernel(tc, tab_words, tab_scales, w4_words, w4_scales,
             )
 
         def finish(s):
-            c0, w = col0[s], width[s]
-            host, a = c_raw[HOSTS[s][0]], FRONT[HOSTS[s][0]] + HOSTS[s][1]
+            c0, w = col0[s], STEPS[s]
+            host, a = c_raw[HOSTS[s][0]], HOSTS[s][1]
             nc.vector.scalar_tensor_tensor(host[:, a : a + w], acc[s][:], bias[:], g_r[:, c0 : c0 + w], ADD, ADD)
             nc.sync.dma_start(out[:, c0 : c0 + w], host[:, a : a + w])
 
+        cast(0)
+        quant(0)
+        nc.vector.tensor_copy(g_r[:], res[:].indirect(offsets[:]))
         for s in range(len(STEPS)):
             open_group(s)
-        for s in range(4):
+        close(0)
+        for s in range(1, len(STEPS)):
             cast(s)
-        for s in range(3):
+        for s in range(1, len(STEPS)):
             quant(s)
-        finish(0)
-        quant(3)
-        cast(4)
-        finish(1)
-        quant(4)
-        finish(2)
-        for s in (5, 6):
-            cast(s)
-        for s in (5, 6):
-            quant(s)
-        for s in range(3, len(STEPS)):
+            close(s)
+            if s == 1:
+                finish(0)
+            if s == 3:
+                finish(1)
+                finish(2)
+            if s == 4:
+                finish(3)
+        for s in range(4, len(STEPS)):
             finish(s)

@@ -19,10 +19,10 @@ P = 128
 PACK = 4
 RUN = 2
 
-LOADS = [256] * 8
+LOADS = [256] * 7 + [128] * 2
 STEPS = [256, 512, 512, 256, 256, 128, 128]
 SHARE = [0, 0, 0, 0, 64, 0, 0]
-HOSTS = [(2, 0), (5, 0), (5, 512), (6, 0), (7, 256), (7, 640), (7, 896)]
+HOSTS = [(2, 0), (4, 0), (5, 0), (6, 0), (8, 0), (8, 256), (8, 384)]
 LAG = 2
 
 
@@ -93,14 +93,14 @@ def tile_list_tabres_bias_kernel(tc, tab_words, tab_scales, w4_words, w4_scales,
         nc.sync.dma_start(res[:], rT)
         load_c(1)
 
+        nc.vector.tensor_copy(*blocks(u_bf[:], u_raw[:]))
+        nc.vector.quantize_mx(u_w[:].bitcast(FP8X4), u_s[:], u_bf[:].rearrange("p n t -> p (n t)"))
         nc.vector.tensor_copy(g_far[:], tab_s[:].bitcast(U8).indirect(offsets[:]))
         for r in range(4):
             nc.sync.dma_start(g_words[r:P:32, :], g_far[:].bitcast(I32)[32 + 4 * r : 96 : 16, :])
         load_c(2)
         load_c(3)
         nc.sync.dma_start(bias[:], b.rearrange("(p o) -> p o", o=1))
-        nc.scalar.copy(*blocks(u_bf[:], u_raw[:]))
-        nc.vector.quantize_mx(u_w[:].bitcast(FP8X4), u_s[:], u_bf[:].rearrange("p n t -> p (n t)"))
         nc.vector.tensor_copy(g_w[:], tab_w[:].bitcast(U32).indirect(offsets[:]))
         for i in range(4, len(LOADS)):
             load_c(i)
@@ -159,12 +159,7 @@ def tile_list_tabres_bias_kernel(tc, tab_words, tab_scales, w4_words, w4_scales,
         for s in range(1, len(STEPS)):
             quant(s)
             close(s)
-            if s == 1:
-                finish(0)
-            if s == 3:
-                finish(1)
-                finish(2)
-            if s == 4:
-                finish(3)
+            if s <= 4:
+                finish(s - 1)
         for s in range(4, len(STEPS)):
             finish(s)

@@ -19,10 +19,10 @@ P = 128
 PACK = 4
 RUN = 2
 
-LOADS = [256] * 7 + [128] * 2
-STEPS = [256, 512, 512, 256, 256, 128, 128]
-SHARE = [0, 0, 0, 0, 64, 0, 0]
-HOSTS = [(2, 0), (4, 0), (5, 0), (6, 0), (8, 0), (8, 256), (8, 384)]
+LOADS = [128] + [256] * 7 + [128]
+STEPS = [128, 512, 512, 256, 256, 256, 128]
+SHARE = [0, 0, 0, 0, 0, 64, 0]
+HOSTS = [(2, 0), (4, 0), (5, 0), (6, 0), (7, 0), (8, 0), (8, 256)]
 LAG = 2
 
 
@@ -38,11 +38,11 @@ def tile_list_tabres_bias_kernel(tc, tab_words, tab_scales, w4_words, w4_scales,
         psum = ctx.enter_context(tc.psum_pool(name="psum", bufs=1))
 
         size = [4 * PACK * w for w in LOADS]
-        at_s = size[2] - 1024
-        at_w = at_s + 2048 + size[3]
-        late = [at_w + sum(size[4:i]) for i in range(4, len(LOADS))]
+        at_s = size[3] - 1024
+        at_w = at_s + 2048 + size[4]
+        late = [at_w + sum(size[5:i]) for i in range(5, len(LOADS))]
         at_0 = max(at_w + 4 * T, late[-1] + size[-1])
-        place = [at_0, at_0 + size[0], 0, at_s + 2048] + late
+        place = [at_0, at_0 + size[0], at_0 + size[0] + size[1], 0, at_s + 2048] + late
 
         offsets = keep.tile([P, S // 16], U16, name="offsets", align_bytes=256)
         tab_w = shared.tile([P, T], I32, name="tab_w", align_bytes=256, offset=at_w)
@@ -86,23 +86,24 @@ def tile_list_tabres_bias_kernel(tc, tab_words, tab_scales, w4_words, w4_scales,
         nc.sync.dma_start(w4_w[:], w4_words[0].bitcast(I32))
         nc.sync.dma_start(tab_s[32:96:4, :], tab_scales[0].bitcast(I32))
         nc.sync.dma_start(tab_w[:], tab_words[0].rearrange("p t i -> p (t i)").bitcast(I32))
+        load_c(0)
+        nc.sync.dma_start(res[:], rT)
         ws_rows = w4_scales[0].bitcast(I32)
         for r in range(4):
             nc.sync.dma_start(w4_s[r:P:32, :], ws_rows[r:16:4, :])
-        load_c(0)
-        nc.sync.dma_start(res[:], rT)
         load_c(1)
+        load_c(2)
 
         nc.vector.tensor_copy(*blocks(u_bf[:], u_raw[:]))
         nc.vector.quantize_mx(u_w[:].bitcast(FP8X4), u_s[:], u_bf[:].rearrange("p n t -> p (n t)"))
         nc.vector.tensor_copy(g_far[:], tab_s[:].bitcast(U8).indirect(offsets[:]))
         for r in range(4):
             nc.sync.dma_start(g_words[r:P:32, :], g_far[:].bitcast(I32)[32 + 4 * r : 96 : 16, :])
-        load_c(2)
         load_c(3)
+        load_c(4)
         nc.sync.dma_start(bias[:], b.rearrange("(p o) -> p o", o=1))
         nc.vector.tensor_copy(g_w[:], tab_w[:].bitcast(U32).indirect(offsets[:]))
-        for i in range(4, len(LOADS)):
+        for i in range(5, len(LOADS)):
             load_c(i)
 
         w4_codes = w4_w[:].bitcast(U8).bitcast(FP4X4)
@@ -159,7 +160,7 @@ def tile_list_tabres_bias_kernel(tc, tab_words, tab_scales, w4_words, w4_scales,
         for s in range(1, len(STEPS)):
             quant(s)
             close(s)
-            if s <= 4:
+            if s <= 5:
                 finish(s - 1)
-        for s in range(4, len(STEPS)):
+        for s in range(5, len(STEPS)):
             finish(s)

@@ -19,10 +19,10 @@ P = 128
 PACK = 4
 RUN = 2
 
-LOADS = [128] + [256] * 7 + [128]
-STEPS = [128, 512, 512, 256, 256, 256, 128]
-SHARE = [0, 0, 0, 0, 0, 64, 0]
-HOSTS = [(2, 0), (4, 0), (5, 0), (6, 0), (7, 0), (8, 0), (8, 256)]
+LOADS = [128, 384, 384, 384, 256, 256, 128, 128]
+STEPS = [512, 512, 256, 256, 256, 128, 128]
+SHARE = [0, 128, 64, 0, 64, 0, 0]
+HOSTS = [(2, 0), (3, 0), (4, 0), (5, 0), (7, 0), (7, 256), (7, 384)]
 LAG = 2
 
 
@@ -150,8 +150,8 @@ def tile_list_tabres_bias_kernel(tc, tab_words, tab_scales, w4_words, w4_scales,
             nc.sync.dma_start(out[:, c0 : c0 + w], host[:, a : a + w])
 
         cast(0)
-        quant(0)
         nc.vector.tensor_copy(g_r[:], res[:].indirect(offsets[:]))
+        quant(0)
         for s in range(len(STEPS)):
             open_group(s)
         close(0)
@@ -160,7 +160,7 @@ def tile_list_tabres_bias_kernel(tc, tab_words, tab_scales, w4_words, w4_scales,
         for s in range(1, len(STEPS)):
             quant(s)
             close(s)
-            if s <= 5:
+            if s <= 4:
                 finish(s - 1)
-        for s in range(5, len(STEPS)):
+        for s in range(4, len(STEPS)):
             finish(s)

@@ -19,10 +19,10 @@ P = 128
 PACK = 4
 RUN = 2
 
-LOADS = [128, 384, 384, 384, 256, 256, 128, 128]
+LOADS = [256] * 7 + [128] * 2
 STEPS = [512, 512, 256, 256, 256, 128, 128]
-SHARE = [0, 128, 64, 0, 64, 0, 0]
-HOSTS = [(2, 0), (3, 0), (4, 0), (5, 0), (7, 0), (7, 256), (7, 384)]
+SHARE = [0, 0, 0, 0, 64, 0, 0]
+HOSTS = [(3, 0), (4, 0), (5, 0), (6, 0), (8, 0), (8, 256), (8, 384)]
 LAG = 2
 
 
@@ -86,22 +86,22 @@ def tile_list_tabres_bias_kernel(tc, tab_words, tab_scales, w4_words, w4_scales,
         nc.sync.dma_start(w4_w[:], w4_words[0].bitcast(I32))
         nc.sync.dma_start(tab_s[32:96:4, :], tab_scales[0].bitcast(I32))
         nc.sync.dma_start(tab_w[:], tab_words[0].rearrange("p t i -> p (t i)").bitcast(I32))
-        load_c(0)
         nc.sync.dma_start(res[:], rT)
         ws_rows = w4_scales[0].bitcast(I32)
         for r in range(4):
             nc.sync.dma_start(w4_s[r:P:32, :], ws_rows[r:16:4, :])
+        load_c(0)
         load_c(1)
         load_c(2)
 
-        nc.vector.tensor_copy(*blocks(u_bf[:], u_raw[:]))
-        nc.vector.quantize_mx(u_w[:].bitcast(FP8X4), u_s[:], u_bf[:].rearrange("p n t -> p (n t)"))
         nc.vector.tensor_copy(g_far[:], tab_s[:].bitcast(U8).indirect(offsets[:]))
         for r in range(4):
             nc.sync.dma_start(g_words[r:P:32, :], g_far[:].bitcast(I32)[32 + 4 * r : 96 : 16, :])
         load_c(3)
         load_c(4)
         nc.sync.dma_start(bias[:], b.rearrange("(p o) -> p o", o=1))
+        nc.scalar.copy(*blocks(u_bf[:], u_raw[:]))
+        nc.vector.quantize_mx(u_w[:].bitcast(FP8X4), u_s[:], u_bf[:].rearrange("p n t -> p (n t)"))
         nc.vector.tensor_copy(g_w[:], tab_w[:].bitcast(U32).indirect(offsets[:]))
         for i in range(5, len(LOADS)):
             load_c(i)

@@ -20,9 +20,9 @@ PACK = 4
 RUN = 2
 
 LOADS = [256] * 7 + [128] * 2
-STEPS = [512, 512, 256, 256, 256, 128, 128]
-SHARE = [0, 0, 0, 0, 64, 0, 0]
-HOSTS = [(3, 0), (4, 0), (5, 0), (6, 0), (8, 0), (8, 256), (8, 384)]
+STEPS = [512, 256, 256, 256, 256, 256, 128, 128]
+SHARE = [0, 0, 0, 0, 0, 128, 0, 0]
+HOSTS = [(2, 0), (3, 0), (4, 0), (5, 0), (6, 0), (8, 0), (8, 256), (8, 384)]
 LAG = 2
 
 
@@ -68,7 +68,7 @@ def tile_list_tabres_bias_kernel(tc, tab_words, tab_scales, w4_words, w4_scales,
         c_s = keep.tile([P, S], U8, name="c_s", align_bytes=256)
         acc = {}
 
-        nc.vector.memset(tab_s[:], 0)
+        nc.vector.memset(tab_s[0:112, :], 0)
         nc.vector.memset(w4_s[:], 0)
         nc.vector.memset(g_words[:], 0)
 
@@ -81,12 +81,12 @@ def tile_list_tabres_bias_kernel(tc, tab_words, tab_scales, w4_words, w4_scales,
             w = LOADS[i]
             nc.sync.dma_start(planes(i), c_rows[:, :, load0[i] : load0[i] + w])
 
+        nc.sync.dma_start(tab_s[112:P, :], tab_scales[0].bitcast(I32))
         nc.sync.dma_start(offsets[:], offs)
-        nc.sync.dma_start(u_raw[:], u.rearrange("(p j) n -> p j n", j=PACK))
-        nc.sync.dma_start(w4_w[:], w4_words[0].bitcast(I32))
-        nc.sync.dma_start(tab_s[32:96:4, :], tab_scales[0].bitcast(I32))
         nc.sync.dma_start(tab_w[:], tab_words[0].rearrange("p t i -> p (t i)").bitcast(I32))
         nc.sync.dma_start(res[:], rT)
+        nc.sync.dma_start(u_raw[:], u.rearrange("(p j) n -> p j n", j=PACK))
+        nc.sync.dma_start(w4_w[:], w4_words[0].bitcast(I32))
         ws_rows = w4_scales[0].bitcast(I32)
         for r in range(4):
             nc.sync.dma_start(w4_s[r:P:32, :], ws_rows[r:16:4, :])
@@ -96,7 +96,7 @@ def tile_list_tabres_bias_kernel(tc, tab_words, tab_scales, w4_words, w4_scales,
 
         nc.vector.tensor_copy(g_far[:], tab_s[:].bitcast(U8).indirect(offsets[:]))
         for r in range(4):
-            nc.sync.dma_start(g_words[r:P:32, :], g_far[:].bitcast(I32)[32 + 4 * r : 96 : 16, :])
+            nc.sync.dma_start(g_words[r:P:32, :], g_far[:].bitcast(I32)[112 + r : P : 4, :])
         load_c(3)
         load_c(4)
         nc.sync.dma_start(bias[:], b.rearrange("(p o) -> p o", o=1))
@@ -111,7 +111,7 @@ def tile_list_tabres_bias_kernel(tc, tab_words, tab_scales, w4_words, w4_scales,
 
         def open_group(s):
             c0, w = col0[s], STEPS[s]
-            acc[s] = psum.tile([P, w], F32, name="acc%d" % s, tag="bank%d" % s)
+            acc[s] = psum.tile([P, w], F32, name="acc%d" % s, tag="bank%d" % (s % 3))
             n = w if w == 512 else 128
             for a in range(0, w, n):
                 nc.tensor.matmul_mx(
@@ -152,7 +152,7 @@ def tile_list_tabres_bias_kernel(tc, tab_words, tab_scales, w4_words, w4_scales,
         cast(0)
         nc.vector.tensor_copy(g_r[:], res[:].indirect(offsets[:]))
         quant(0)
-        for s in range(len(STEPS)):
+        for s in range(3):
             open_group(s)
         close(0)
         for s in range(1, len(STEPS)):
@@ -160,7 +160,8 @@ def tile_list_tabres_bias_kernel(tc, tab_words, tab_scales, w4_words, w4_scales,
         for s in range(1, len(STEPS)):
             quant(s)
             close(s)
-            if s <= 4:
+            if s <= 5:
                 finish(s - 1)
-        for s in range(4, len(STEPS)):
+                open_group(s + 2)
+        for s in range(5, len(STEPS)):
             finish(s)

@@ -14,16 +14,17 @@ U8 = mybir.dt.uint8
 FP8X4 = mybir.dt.float8_e4m3fn_x4
 FP4X4 = mybir.dt.float4_e2m1fn_x4
 ADD = mybir.AluOpType.add
+MULT = mybir.AluOpType.mult
 
 P = 128
 PACK = 4
 RUN = 2
 
-LOADS = [256] * 7 + [128] * 2
+LOADS = [512] + [256] * 5 + [128] * 2
 STEPS = [512, 256, 256, 256, 256, 256, 128, 128]
 SHARE = [0, 0, 0, 0, 0, 128, 0, 0]
-HOSTS = [(2, 0), (3, 0), (4, 0), (5, 0), (6, 0), (8, 0), (8, 256), (8, 384)]
-LAG = 2
+HOSTS = [(1, 0), (2, 0), (3, 0), (4, 0), (5, 0), (7, 0), (7, 256), (7, 384)]
+EARLY = 2
 
 
 def blocks(dst, src):
@@ -38,11 +39,11 @@ def tile_list_tabres_bias_kernel(tc, tab_words, tab_scales, w4_words, w4_scales,
         psum = ctx.enter_context(tc.psum_pool(name="psum", bufs=1))
 
         size = [4 * PACK * w for w in LOADS]
-        at_s = size[3] - 1024
-        at_w = at_s + 2048 + size[4]
-        late = [at_w + sum(size[5:i]) for i in range(5, len(LOADS))]
+        at_s = size[EARLY] - 1024
+        at_w = at_s + 2048 + size[EARLY + 1]
+        late = [at_w + sum(size[EARLY + 2 : i]) for i in range(EARLY + 2, len(LOADS))]
         at_0 = max(at_w + 4 * T, late[-1] + size[-1])
-        place = [at_0, at_0 + size[0], at_0 + size[0] + size[1], 0, at_s + 2048] + late
+        place = [at_0 + sum(size[:i]) for i in range(EARLY)] + [0, at_s + 2048] + late
 
         offsets = keep.tile([P, S // 16], U16, name="offsets", align_bytes=256)
         tab_w = shared.tile([P, T], I32, name="tab_w", align_bytes=256, offset=at_w)
@@ -90,20 +91,19 @@ def tile_list_tabres_bias_kernel(tc, tab_words, tab_scales, w4_words, w4_scales,
         ws_rows = w4_scales[0].bitcast(I32)
         for r in range(4):
             nc.sync.dma_start(w4_s[r:P:32, :], ws_rows[r:16:4, :])
-        load_c(0)
-        load_c(1)
-        load_c(2)
+        for i in range(EARLY):
+            load_c(i)
 
         nc.vector.tensor_copy(g_far[:], tab_s[:].bitcast(U8).indirect(offsets[:]))
         for r in range(4):
             nc.sync.dma_start(g_words[r:P:32, :], g_far[:].bitcast(I32)[112 + r : P : 4, :])
-        load_c(3)
-        load_c(4)
+        load_c(EARLY)
+        load_c(EARLY + 1)
         nc.sync.dma_start(bias[:], b.rearrange("(p o) -> p o", o=1))
         nc.scalar.copy(*blocks(u_bf[:], u_raw[:]))
         nc.vector.quantize_mx(u_w[:].bitcast(FP8X4), u_s[:], u_bf[:].rearrange("p n t -> p (n t)"))
         nc.vector.tensor_copy(g_w[:], tab_w[:].bitcast(U32).indirect(offsets[:]))
-        for i in range(5, len(LOADS)):
+        for i in range(EARLY + 2, len(LOADS)):
             load_c(i)
 
         w4_codes = w4_w[:].bitcast(U8).bitcast(FP4X4)
@@ -126,6 +126,11 @@ def tile_list_tabres_bias_kernel(tc, tab_words, tab_scales, w4_words, w4_scales,
             for copy, lo, hi in ((nc.scalar.copy, c0, cut), (nc.vector.tensor_copy, cut, c0 + STEPS[s])):
                 for i, w in enumerate(LOADS):
                     a, e = max(lo, load0[i]), min(hi, load0[i] + w)
+                    if a < e and i == 0:
+                        e = w // 2
+                        nc.gpsimd.tensor_scalar(
+                            c_bf[0][:, e:w, :], planes(0)[:, :, e:w].rearrange("p t n -> p n t"), 1.0, 0.0, MULT, ADD
+                        )
                     if a < e:
                         copy(*blocks(c_bf[s][:, a - c0 : e - c0, :], planes(i)[:, :, a - load0[i] : e - load0[i]]))
 

@@ -25,6 +25,7 @@ STEPS = [512, 256, 256, 256, 256, 256, 128, 128]
 SHARE = [0, 0, 0, 0, 0, 128, 0, 0]
 HOSTS = [(1, 0), (2, 0), (3, 0), (4, 0), (5, 0), (7, 0), (7, 256), (7, 384)]
 EARLY = 2
+POOL_SHARE = [256, 96]
 
 
 def blocks(dst, src):
@@ -126,10 +127,11 @@ def tile_list_tabres_bias_kernel(tc, tab_words, tab_scales, w4_words, w4_scales,
             for copy, lo, hi in ((nc.scalar.copy, c0, cut), (nc.vector.tensor_copy, cut, c0 + STEPS[s])):
                 for i, w in enumerate(LOADS):
                     a, e = max(lo, load0[i]), min(hi, load0[i] + w)
-                    if a < e and i == 0:
-                        e = w // 2
+                    if a < e and i < len(POOL_SHARE):
+                        e = e - POOL_SHARE[i]
+                        cut_at = w - POOL_SHARE[i]
                         nc.gpsimd.tensor_scalar(
-                            c_bf[0][:, e:w, :], planes(0)[:, :, e:w].rearrange("p t n -> p n t"), 1.0, 0.0, MULT, ADD
+                            c_bf[i][:, cut_at:w, :], planes(i)[:, :, cut_at:w].rearrange("p t n -> p n t"), 1.0, 0.0, MULT, ADD
                         )
                     if a < e:
                         copy(*blocks(c_bf[s][:, a - c0 : e - c0, :], planes(i)[:, :, a - load0[i] : e - load0[i]]))

@@ -23,8 +23,9 @@ RUN = 2
 LOADS = [512] + [256] * 5 + [128] * 2
 STEPS = [512, 256, 256, 256, 256, 256, 128, 128]
 SHARE = [0, 0, 0, 0, 0, 128, 0, 0]
-HOSTS = [(1, 0), (2, 0), (3, 0), (4, 0), (5, 0), (7, 0), (7, 256), (7, 384)]
+HOSTS = [(1, 0), (2, 0), (2, 256), (4, 0), (5, 0), (7, 0), (7, 256), (7, 384)]
 EARLY = 2
+BANK = [0, 1, 2, 0, 1, 0, 2, 1]
 POOL_SHARE = [256, 96]
 
 
@@ -112,7 +113,7 @@ def tile_list_tabres_bias_kernel(tc, tab_words, tab_scales, w4_words, w4_scales,
 
         def open_group(s):
             c0, w = col0[s], STEPS[s]
-            acc[s] = psum.tile([P, w], F32, name="acc%d" % s, tag="bank%d" % (s % 3))
+            acc[s] = psum.tile([P, w], F32, name="acc%d" % s, tag="bank%d" % BANK[s])
             n = w if w == 512 else 128
             for a in range(0, w, n):
                 nc.tensor.matmul_mx(
@@ -164,11 +165,12 @@ def tile_list_tabres_bias_kernel(tc, tab_words, tab_scales, w4_words, w4_scales,
         close(0)
         for s in range(1, len(STEPS)):
             cast(s)
+        heir = {0: 3, 1: 4, 2: 6, 3: 5, 4: 7}
         for s in range(1, len(STEPS)):
             quant(s)
             close(s)
-            if s <= 5:
-                finish(s - 1)
-                open_group(s + 2)
+            for done in {1: [0], 2: [1, 2], 4: [3], 5: [4]}.get(s, []):
+                finish(done)
+                open_group(heir[done])
         for s in range(5, len(STEPS)):
             finish(s)

@@ -21,12 +21,12 @@ PACK = 4
 RUN = 2
 
 LOADS = [512] + [256] * 5 + [128] * 2
-STEPS = [512, 256, 256, 256, 256, 256, 128, 128]
+STEPS = [384, 384, 256, 256, 256, 256, 128, 128]
 SHARE = [0, 0, 0, 0, 0, 128, 0, 0]
-HOSTS = [(1, 0), (2, 0), (2, 256), (4, 0), (5, 0), (7, 0), (7, 256), (7, 384)]
+HOSTS = [(1, 0), (2, 0), (2, 384), (4, 0), (5, 0), (7, 0), (7, 256), (7, 384)]
 EARLY = 2
 BANK = [0, 1, 2, 0, 1, 0, 2, 1]
-POOL_SHARE = [256, 96]
+POOL_SHARE = [256, 96, 0, 0, 0, 0, 0, 48]
 
 
 def blocks(dst, src):
@@ -56,9 +56,6 @@ def tile_list_tabres_bias_kernel(tc, tab_words, tab_scales, w4_words, w4_scales,
         res = keep.tile([P, T], F32, name="res", align_bytes=256)
         w4_w = keep.tile([P, 2 * M // 4], I32, name="w4_w", align_bytes=256)
         u_raw = keep.tile([P, PACK, M], F32, name="u_raw", align_bytes=256)
-        u_bf = keep.tile([P, M, PACK], BF16, name="u_bf", align_bytes=256)
-        u_w = keep.tile([P, M], U32, name="u_w", align_bytes=256)
-        u_s = keep.tile([P, M], U8, name="u_s", align_bytes=256)
         g_w = keep.tile([P, S], U32, name="g_w", align_bytes=256)
         g_far = keep.tile([P, S], U8, name="g_far", align_bytes=256)
         g_words = keep.tile([P, S // 4], I32, name="g_words", align_bytes=256)
@@ -66,9 +63,9 @@ def tile_list_tabres_bias_kernel(tc, tab_words, tab_scales, w4_words, w4_scales,
         g_r = keep.tile([P, S], F32, name="g_r", align_bytes=256)
         load0 = [sum(LOADS[:i]) for i in range(len(LOADS))]
         col0 = [sum(STEPS[:s]) for s in range(len(STEPS))]
-        c_bf = [keep.tile([P, w, PACK], BF16, name="c_bf%d" % s, align_bytes=256) for s, w in enumerate(STEPS)]
-        c_w = keep.tile([P, S], U32, name="c_w", align_bytes=256)
-        c_s = keep.tile([P, S], U8, name="c_s", align_bytes=256)
+        x_bf = keep.tile([P, M + S, PACK], BF16, name="x_bf", align_bytes=256)
+        x_w = keep.tile([P, M + S], U32, name="x_w", align_bytes=256)
+        x_s = keep.tile([P, M + S], U8, name="x_s", align_bytes=256)
         acc = {}
 
         nc.vector.memset(tab_s[0:112, :], 0)
@@ -102,8 +99,7 @@ def tile_list_tabres_bias_kernel(tc, tab_words, tab_scales, w4_words, w4_scales,
         load_c(EARLY)
         load_c(EARLY + 1)
         nc.sync.dma_start(bias[:], b.rearrange("(p o) -> p o", o=1))
-        nc.scalar.copy(*blocks(u_bf[:], u_raw[:]))
-        nc.vector.quantize_mx(u_w[:].bitcast(FP8X4), u_s[:], u_bf[:].rearrange("p n t -> p (n t)"))
+        nc.scalar.copy(*blocks(x_bf[:, 0:M, :], u_raw[:]))
         nc.vector.tensor_copy(g_w[:], tab_w[:].bitcast(U32).indirect(offsets[:]))
         for i in range(EARLY + 2, len(LOADS)):
             load_c(i)
@@ -111,45 +107,45 @@ def tile_list_tabres_bias_kernel(tc, tab_words, tab_scales, w4_words, w4_scales,
         w4_codes = w4_w[:].bitcast(U8).bitcast(FP4X4)
         w4_scale = w4_s[:].bitcast(U8)
 
+        def pieces(w, n):
+            return [(a, min(n, w - a)) for a in range(0, w, n)]
+
         def open_group(s):
             c0, w = col0[s], STEPS[s]
             acc[s] = psum.tile([P, w], F32, name="acc%d" % s, tag="bank%d" % BANK[s])
-            n = w if w == 512 else 128
-            for a in range(0, w, n):
+            for a, n in pieces(w, 128):
                 nc.tensor.matmul_mx(
                     acc[s][:, a : a + n], lhsT=w4_codes, lhsT_scale=w4_scale,
                     rhs=g_w[:, c0 + a : c0 + a + n].bitcast(FP8X4), rhs_scale=g_s[:, c0 + a : c0 + a + n],
                     start=a == 0, stop=False,
                 )
 
-        def cast(s):
-            c0 = col0[s]
-            cut = c0 + STEPS[s] - SHARE[s]
-            for copy, lo, hi in ((nc.scalar.copy, c0, cut), (nc.vector.tensor_copy, cut, c0 + STEPS[s])):
-                for i, w in enumerate(LOADS):
-                    a, e = max(lo, load0[i]), min(hi, load0[i] + w)
-                    if a < e and i < len(POOL_SHARE):
-                        e = e - POOL_SHARE[i]
-                        cut_at = w - POOL_SHARE[i]
-                        nc.gpsimd.tensor_scalar(
-                            c_bf[i][:, cut_at:w, :], planes(i)[:, :, cut_at:w].rearrange("p t n -> p n t"), 1.0, 0.0, MULT, ADD
-                        )
-                    if a < e:
-                        copy(*blocks(c_bf[s][:, a - c0 : e - c0, :], planes(i)[:, :, a - load0[i] : e - load0[i]]))
+        def cast(i):
+            w, x0 = LOADS[i], M + load0[i]
+            pool = POOL_SHARE[i] if i < len(POOL_SHARE) else 0
+            cut = w - pool - SHARE[i]
+            if pool:
+                nc.gpsimd.tensor_scalar(
+                    x_bf[:, x0 + cut : x0 + w, :], planes(i)[:, :, cut:w].rearrange("p t n -> p n t"), 1.0, 0.0, MULT, ADD
+                )
+            nc.scalar.copy(*blocks(x_bf[:, x0 : x0 + cut, :], planes(i)[:, :, 0:cut]))
+            if SHARE[i]:
+                nc.vector.tensor_copy(*blocks(x_bf[:, x0 + cut : x0 + w, :], planes(i)[:, :, cut:w]))
 
         def quant(s):
-            c0, w = col0[s], STEPS[s]
+            lo, hi = (M + col0[s] if s else 0), M + col0[s] + STEPS[s]
             nc.vector.quantize_mx(
-                c_w[:, c0 : c0 + w].bitcast(FP8X4), c_s[:, c0 : c0 + w], c_bf[s][:].rearrange("p n t -> p (n t)")
+                x_w[:, lo:hi].bitcast(FP8X4), x_s[:, lo:hi], x_bf[:, lo:hi, :].rearrange("p n t -> p (n t)")
             )
 
         def close(s):
-            c0, w = col0[s], STEPS[s]
-            nc.tensor.matmul_mx(
-                acc[s][:], lhsT=u_w[:].bitcast(FP8X4), lhsT_scale=u_s[:],
-                rhs=c_w[:, c0 : c0 + w].bitcast(FP8X4), rhs_scale=c_s[:, c0 : c0 + w],
-                start=False, stop=True,
-            )
+            x0, w = M + col0[s], STEPS[s]
+            for a, n in pieces(w, 256):
+                nc.tensor.matmul_mx(
+                    acc[s][:, a : a + n], lhsT=x_w[:, 0:M].bitcast(FP8X4), lhsT_scale=x_s[:, 0:M],
+                    rhs=x_w[:, x0 + a : x0 + a + n].bitcast(FP8X4), rhs_scale=x_s[:, x0 + a : x0 + a + n],
+                    start=False, stop=a + n == w,
+                )
 
         def finish(s):
             c0, w = col0[s], STEPS[s]

from contextlib import ExitStack

import concourse.mybir as mybir

K, M, T, S = 512, 128, 4096, 2048
FLOPS = 2 * 2 * K * M * S

F32 = mybir.dt.float32
BF16 = mybir.dt.bfloat16
I32 = mybir.dt.int32
U32 = mybir.dt.uint32
U16 = mybir.dt.uint16
U8 = mybir.dt.uint8
FP8X4 = mybir.dt.float8_e4m3fn_x4
FP4X4 = mybir.dt.float4_e2m1fn_x4
ADD = mybir.AluOpType.add
MULT = mybir.AluOpType.mult

P = 128
PACK = 4
RUN = 2

LOADS = [512] + [256] * 5 + [128] * 2
STEPS = [384, 384, 256, 256, 256, 256, 128, 128]
SHARE = [0, 0, 0, 0, 0, 128, 0, 0]
HOSTS = [(1, 0), (2, 0), (2, 384), (4, 0), (5, 0), (7, 0), (7, 256), (7, 384)]
EARLY = 2
BANK = [0, 1, 2, 0, 1, 0, 2, 1]
POOL_SHARE = [256, 96, 0, 0, 0, 0, 0, 48]


def blocks(dst, src):
    return dst.rearrange("p (c i) t -> p c t i", i=RUN), src.rearrange("p t (c i) -> p c t i", i=RUN)


def tile_list_tabres_bias_kernel(tc, tab_words, tab_scales, w4_words, w4_scales, c, u, rT, b, offs, out):
    nc = tc.nc
    with ExitStack() as ctx:
        keep = ctx.enter_context(tc.tile_pool(name="keep", bufs=1))
        shared = ctx.enter_context(tc.tile_pool(name="shared", bufs=1))
        psum = ctx.enter_context(tc.psum_pool(name="psum", bufs=1))

        size = [4 * PACK * w for w in LOADS]
        at_s = size[EARLY] - 1024
        at_w = at_s + 2048 + size[EARLY + 1]
        late = [at_w + sum(size[EARLY + 2 : i]) for i in range(EARLY + 2, len(LOADS))]
        at_0 = max(at_w + 4 * T, late[-1] + size[-1])
        place = [at_0 + sum(size[:i]) for i in range(EARLY)] + [0, at_s + 2048] + late

        offsets = keep.tile([P, S // 16], U16, name="offsets", align_bytes=256)
        tab_w = shared.tile([P, T], I32, name="tab_w", align_bytes=256, offset=at_w)
        tab_s = shared.tile([P, T // 4], I32, name="tab_s", align_bytes=256, offset=at_s)
        w4_s = keep.tile([P, M // 4], I32, name="w4_s", align_bytes=256)
        bias = shared.tile([P, 1], F32, name="bias", align_bytes=256, offset=at_s + 1280)
        c_raw = [shared.tile([P, PACK * w], F32, name="c_raw%d" % i, align_bytes=256, offset=place[i]) for i, w in enumerate(LOADS)]
        res = keep.tile([P, T], F32, name="res", align_bytes=256)
        w4_w = keep.tile([P, 2 * M // 4], I32, name="w4_w", align_bytes=256)
        u_raw = keep.tile([P, PACK, M], F32, name="u_raw", align_bytes=256)
        g_w = keep.tile([P, S], U32, name="g_w", align_bytes=256)
        g_far = keep.tile([P, S], U8, name="g_far", align_bytes=256)
        g_words = keep.tile([P, S // 4], I32, name="g_words", align_bytes=256)
        g_s = g_words[:].bitcast(U8)
        g_r = keep.tile([P, S], F32, name="g_r", align_bytes=256)
        load0 = [sum(LOADS[:i]) for i in range(len(LOADS))]
        col0 = [sum(STEPS[:s]) for s in range(len(STEPS))]
        x_bf = keep.tile([P, M + S, PACK], BF16, name="x_bf", align_bytes=256)
        x_w = keep.tile([P, M + S], U32, name="x_w", align_bytes=256)
        x_s = keep.tile([P, M + S], U8, name="x_s", align_bytes=256)
        acc = {}

        nc.vector.memset(tab_s[0:112, :], 0)
        nc.vector.memset(w4_s[:], 0)
        nc.vector.memset(g_words[:], 0)

        c_rows = c.rearrange("(p j) s -> p j s", j=PACK)

        def planes(i):
            return c_raw[i][:].rearrange("p (j s) -> p j s", j=PACK)

        def load_c(i):
            w = LOADS[i]
            nc.sync.dma_start(planes(i), c_rows[:, :, load0[i] : load0[i] + w])

        nc.sync.dma_start(tab_s[112:P, :], tab_scales[0].bitcast(I32))
        nc.sync.dma_start(offsets[:], offs)
        nc.sync.dma_start(tab_w[:], tab_words[0].rearrange("p t i -> p (t i)").bitcast(I32))
        nc.sync.dma_start(res[:], rT)
        nc.sync.dma_start(u_raw[:], u.rearrange("(p j) n -> p j n", j=PACK))
        nc.sync.dma_start(w4_w[:], w4_words[0].bitcast(I32))
        ws_rows = w4_scales[0].bitcast(I32)
        for r in range(4):
            nc.sync.dma_start(w4_s[r:P:32, :], ws_rows[r:16:4, :])
        for i in range(EARLY):
            load_c(i)

        nc.vector.tensor_copy(g_far[:], tab_s[:].bitcast(U8).indirect(offsets[:]))
        for r in range(4):
            nc.sync.dma_start(g_words[r:P:32, :], g_far[:].bitcast(I32)[112 + r : P : 4, :])
        load_c(EARLY)
        load_c(EARLY + 1)
        nc.sync.dma_start(bias[:], b.rearrange("(p o) -> p o", o=1))
        nc.scalar.copy(*blocks(x_bf[:, 0:M, :], u_raw[:]))
        nc.vector.tensor_copy(g_w[:], tab_w[:].bitcast(U32).indirect(offsets[:]))
        for i in range(EARLY + 2, len(LOADS)):
            load_c(i)

        w4_codes = w4_w[:].bitcast(U8).bitcast(FP4X4)
        w4_scale = w4_s[:].bitcast(U8)

        def pieces(w, n):
            return [(a, min(n, w - a)) for a in range(0, w, n)]

        def open_group(s):
            c0, w = col0[s], STEPS[s]
            acc[s] = psum.tile([P, w], F32, name="acc%d" % s, tag="bank%d" % BANK[s])
            for a, n in pieces(w, 128):
                nc.tensor.matmul_mx(
                    acc[s][:, a : a + n], lhsT=w4_codes, lhsT_scale=w4_scale,
                    rhs=g_w[:, c0 + a : c0 + a + n].bitcast(FP8X4), rhs_scale=g_s[:, c0 + a : c0 + a + n],
                    start=a == 0, stop=False,
                )

        def cast(i):
            w, x0 = LOADS[i], M + load0[i]
            pool = POOL_SHARE[i] if i < len(POOL_SHARE) else 0
            cut = w - pool - SHARE[i]
            if pool:
                nc.gpsimd.tensor_scalar(
                    x_bf[:, x0 + cut : x0 + w, :], planes(i)[:, :, cut:w].rearrange("p t n -> p n t"), 1.0, 0.0, MULT, ADD
                )
            nc.scalar.copy(*blocks(x_bf[:, x0 : x0 + cut, :], planes(i)[:, :, 0:cut]))
            if SHARE[i]:
                nc.vector.tensor_copy(*blocks(x_bf[:, x0 + cut : x0 + w, :], planes(i)[:, :, cut:w]))

        def quant(s):
            lo, hi = (M + col0[s] if s else 0), M + col0[s] + STEPS[s]
            nc.vector.quantize_mx(
                x_w[:, lo:hi].bitcast(FP8X4), x_s[:, lo:hi], x_bf[:, lo:hi, :].rearrange("p n t -> p (n t)")
            )

        def close(s):
            x0, w = M + col0[s], STEPS[s]
            for a, n in pieces(w, 256):
                nc.tensor.matmul_mx(
                    acc[s][:, a : a + n], lhsT=x_w[:, 0:M].bitcast(FP8X4), lhsT_scale=x_s[:, 0:M],
                    rhs=x_w[:, x0 + a : x0 + a + n].bitcast(FP8X4), rhs_scale=x_s[:, x0 + a : x0 + a + n],
                    start=False, stop=a + n == w,
                )

        def finish(s):
            c0, w = col0[s], STEPS[s]
            host, a = c_raw[HOSTS[s][0]], HOSTS[s][1]
            nc.vector.scalar_tensor_tensor(host[:, a : a + w], acc[s][:], bias[:], g_r[:, c0 : c0 + w], ADD, ADD)
            nc.sync.dma_start(out[:, c0 : c0 + w], host[:, a : a + w])

        cast(0)
        nc.vector.tensor_copy(g_r[:], res[:].indirect(offsets[:]))
        quant(0)
        for s in range(3):
            open_group(s)
        close(0)
        for s in range(1, len(STEPS)):
            cast(s)
        heir = {0: 3, 1: 4, 2: 6, 3: 5, 4: 7}
        for s in range(1, len(STEPS)):
            quant(s)
            close(s)
            for done in {1: [0], 2: [1, 2], 4: [3], 5: [4]}.get(s, []):
                finish(done)
                open_group(heir[done])
        for s in range(5, len(STEPS)):
            finish(s)
